import numpy as np
import ml_dtypes


def mxq(x, axis, fmt="e4m3"):
    dtype, down = {"e4m3": (ml_dtypes.float8_e4m3fn, 7), "e5m2": (ml_dtypes.float8_e5m2, 14)}[fmt]
    v = np.moveaxis(np.asarray(x, np.float32).astype(ml_dtypes.bfloat16).astype(np.float64), axis, -1)
    blocks = v.reshape(v.shape[:-1] + (-1, 32))
    amax = np.abs(blocks).max(-1, keepdims=True)
    byte = np.maximum(np.where(amax > 0, np.frexp(amax)[1] - 1 + 127, 0) - down, 1)
    scale = np.exp2(byte - 127.0)
    codes = (blocks / scale).astype(np.float32).astype(dtype).astype(np.float64)
    return np.moveaxis((codes * scale).reshape(v.shape), -1, axis)


WIDE = False


def mx_kscale(k):
    if not WIDE:
        return np.ones(k)
    levels = np.array([10, -10, 5, -5, 0])
    if k % 512:
        return np.exp2(np.random.permutation(np.resize(levels, k // 32))).repeat(32)
    a = np.empty((k // 512, 16))
    for p in range(k // 512):
        a[p, :8] = np.random.permutation(np.resize(levels, 8))
        for g in range(8):
            far = levels[np.abs(levels - a[p, g]) >= 10]
            a[p, g + 8] = far[np.random.randint(len(far))]
    return np.exp2(a.ravel()).repeat(32)


def f64(x):
    return np.asarray(x).astype(np.float64)


def striped(idx):
    return np.tile(idx.reshape(-1, 16).T, (8, 1)).astype(np.uint16)


def unstriped(offs):
    return offs[:16].T.reshape(-1).astype(np.int64)


E2M1 = np.array([0.0, 0.5, 1.0, 1.5, 2.0, 3.0, 4.0, 6.0, -0.0, -0.5, -1.0, -1.5, -2.0, -3.0, -4.0, -6.0])


def pack_weight(w, fmt):
    k, n = w.shape
    w = f64(np.asarray(w, np.float32).astype(ml_dtypes.bfloat16)).reshape(k // 32, 32, n)
    amax = np.abs(w).max(1)
    if fmt == "e4m3":
        byte = np.frexp(amax)[1] - 1 + 127 - 7
    else:
        mant, ex = np.frexp(amax / 6.0)
        byte = np.where(mant > 0.5, ex, ex - 1) + 127
    byte = np.clip(np.where(amax > 0, byte, 1), 1, 254)
    scaled = (w * np.exp2(127.0 - byte)[:, None, :]).reshape(k, n).astype(np.float32)
    by_word = np.ascontiguousarray(scaled.reshape(k // 512, 128, 4, n).transpose(0, 1, 3, 2))
    if fmt == "e4m3":
        words = by_word.astype(ml_dtypes.float8_e4m3fn).view(np.uint8)
    else:
        c = by_word.astype(ml_dtypes.float4_e2m1fn).view(np.uint8) & 0xF
        words = (c[..., 0::2] | (c[..., 1::2] << 4)).reshape(k // 512, 128, 2 * n)
    return np.ascontiguousarray(words), np.ascontiguousarray(byte.astype(np.uint8).reshape(k // 512, 16, n))


def unpack_weight(words, scales, fmt):
    g, _, n = scales.shape
    words = np.ascontiguousarray(words).reshape(g, 128, n, -1)
    if fmt == "e4m3":
        vals = words.view(ml_dtypes.float8_e4m3fn).astype(np.float64)
    else:
        nib = np.empty((g, 128, n, 4), np.uint8)
        nib[..., 0::2] = words & 0xF
        nib[..., 1::2] = words >> 4
        vals = E2M1[nib]
    vals = vals * np.repeat(np.exp2(scales.astype(np.float64) - 127.0), 8, axis=1)[..., None]
    return vals.transpose(0, 1, 3, 2).reshape(g * 512, n)


def gelu(v):
    return 0.5 * v * (1.0 + np.tanh(np.sqrt(2.0 / np.pi) * (v + 0.044715 * v**3)))


def often(T, S):
    return np.random.permutation(T)[(T * np.random.uniform(0, 1, S) ** 4).astype(np.int64)]


K, H, N, T, T2, S, P = 1024, 1024, 512, 2048, 2048, 1024, 512


def setup_inputs():
    n = np.random.standard_normal
    s = mx_kscale(K)[:, None]
    u = mx_kscale(H)[:, None]
    tab_words, tab_scales = pack_weight(n((K, T)) * s, "e4m3")
    tab2_words, tab2_scales = pack_weight(n((K, T2)) * s, "e4m3")
    wc_words, wc_scales = pack_weight(n((K, H)) / np.sqrt(K) / s, "e2m1")
    wo_words, wo_scales = pack_weight(n((H, N)) / np.sqrt(H) / u, "e4m3")
    return {
        "tab_words": tab_words, "tab_scales": tab_scales,
        "offs": striped(np.random.permutation(T)[:S]),
        "pos1": striped(often(S, P)),
        "tab2_words": tab2_words, "tab2_scales": tab2_scales,
        "offs2": striped(np.random.permutation(T2)[:P]),
        "wc_words": wc_words, "wc_scales": wc_scales,
        "wf": (n((K, H)) / np.sqrt(K) / s).astype(np.float32),
        "wo_words": wo_words, "wo_scales": wo_scales,
        "level": (np.exp(0.3 * n(H)) * u[:, 0]).astype(np.float32),
        "fade": (np.random.uniform(0.5, 1.5, H) * u[:, 0]).astype(np.float32),
        "base": n((N, P)).astype(np.float32),
    }


def reference(tab_words, tab_scales, offs, pos1, tab2_words, tab2_scales, offs2,
              wc_words, wc_scales, wf, wo_words, wo_scales, level, fade, base):
    v = unpack_weight(tab_words, tab_scales, "e4m3")[:, unstriped(offs)]
    v2 = unpack_weight(tab2_words, tab2_scales, "e4m3")[:, unstriped(offs2)]
    coarse = unpack_weight(wc_words, wc_scales, "e2m1").T @ v
    fine = mxq(f64(wf), 0, "e4m3").T @ v2
    a = coarse[:, unstriped(pos1)]
    z = f64(level)[:, None] * a + f64(fade)[:, None] * np.tanh(fine - a)
    y = unpack_weight(wo_words, wo_scales, "e4m3").T @ mxq(z, 0, "e4m3")
    return y + f64(base)

@@ -1,0 +1,354 @@
+from contextlib import ExitStack
+
+import concourse.mybir as mybir
+
+K, H, N, T, S, M = 1024, 1024, 512, 2048, 1024, 512
+FLOPS = 2 * K * H * S + 2 * K * H * M + 2 * H * N * M
+
+F32 = mybir.dt.float32
+BF16 = mybir.dt.bfloat16
+I32 = mybir.dt.int32
+U32 = mybir.dt.uint32
+U16 = mybir.dt.uint16
+U8 = mybir.dt.uint8
+FP8X4 = mybir.dt.float8_e4m3fn_x4
+FP4X4 = mybir.dt.float4_e2m1fn_x4
+ACT = mybir.ActivationFunctionType
+ALU = mybir.AluOpType
+
+P = 128
+PACK = 4
+PASS = P * PACK
+BANK = 512
+HALF = M // 2
+QUADS = 4
+DEAD = 24
+
+
+def tile_list_lunar_tile_morph_kernel(
+    tc, tab_words, tab_scales, offs, pos1, tab2_words, tab2_scales, offs2,
+    wc_words, wc_scales, wf, wo_words, wo_scales, level, fade, base, out,
+):
+    nc = tc.nc
+    with ExitStack() as ctx:
+        keep = ctx.enter_context(tc.tile_pool(name="keep", bufs=1))
+        psum = ctx.enter_context(tc.psum_pool(name="psum", bufs=4))
+
+        def sb(name, shape, dtype):
+            return keep.tile(shape, dtype, name=name, align_bytes=64)
+
+        def staged(name, slot, shape, dtype):
+            return keep.tile(shape, dtype, name=name, tag="stage%d" % slot, bufs=1, align_bytes=64)
+
+        def zero(engine, tile):
+            engine.memset(tile[:].bitcast(I32), 0)
+
+        def load_planes_packed(tile, first, scales):
+            for q in range(QUADS):
+                nc.sync.dma_start(
+                    out=tile[32 * q + first : 32 * q + first + 8, :].bitcast(I32),
+                    in_=scales[:, 4 * q : 4 * q + 4, :].bitcast(I32),
+                )
+
+        def load_words(tile, words):
+            nc.sync.dma_start(out=tile[:].bitcast(I32), in_=words.rearrange("p t i -> p (t i)").bitcast(I32))
+
+        offs_t = keep.tile([P, S // 16], U16, name="offs_t")
+        pos_t = keep.tile([P, M // 16], U16, name="pos_t")
+        offs2_t = keep.tile([P, M // 16], U16, name="offs2_t")
+
+        tab_sc = sb("tab_sc", [P, T], U8)
+        wc_sc_raw = sb("wc_sc_raw", [P, 2 * H], U8)
+        tab2_sc = sb("tab2_sc", [P, T], U8)
+        v_sc = [sb("v_sc%d" % a, [P, S], U8) for a in range(2)]
+        wo_sc = sb("wo_sc", [P, N], U8)
+        zero(nc.vector, wc_sc_raw)
+        for q in range(QUADS):
+            zero(nc.vector, tab_sc[32 * q : 32 * q + DEAD, :])
+        for tile in (v_sc[0], v_sc[1], tab2_sc, wo_sc):
+            zero(nc.gpsimd, tile)
+
+        nc.sync.dma_start(offs_t[:], offs)
+        load_planes_packed(tab_sc, DEAD, tab_scales)
+        wc_raw = sb("wc_raw", [P, 2 * 2 * H], U8)
+        nc.sync.dma_start(
+            out=wc_raw[:].bitcast(I32).rearrange("p (a c) -> p a c", a=2),
+            in_=wc_words.bitcast(I32).rearrange("a p c -> p a c"),
+        )
+        tab_w = [staged("tab_w%d" % a, a, [P, T], U32) for a in range(2)]
+        load_words(tab_w[0], tab_words[0])
+        nc.sync.dma_start(offs2_t[:], offs2)
+        for q in range(QUADS):
+            nc.sync.dma_start(
+                out=wc_sc_raw[32 * q : 32 * q + 4, :].bitcast(I32).rearrange("r (a c) -> r a c", a=2),
+                in_=wc_scales[:, 4 * q : 4 * q + 4, :].bitcast(I32).rearrange("a r c -> r a c"),
+            )
+        load_words(tab_w[1], tab_words[1])
+        nc.sync.dma_start(pos_t[:], pos1)
+        level_t = sb("level_t", [P, 2, PACK], F32)
+        fade_t = sb("fade_t", [P, 2, PACK], F32)
+
+        def load_factors():
+            nc.sync.dma_start(out=level_t[:], in_=level.rearrange("(b p t) -> p b t", b=2, t=PACK))
+            nc.sync.dma_start(out=fade_t[:], in_=fade.rearrange("(b p t) -> p b t", b=2, t=PACK))
+
+        wf_raw, tab2_w, late = {}, {}, {}
+
+        def load_wf(a, b, slot):
+            wf_raw[a, b] = staged("wf_raw%d%d" % (a, b), slot, [P, PACK, PASS], F32)
+            nc.sync.dma_start(
+                out=wf_raw[a, b][:],
+                in_=wf[PASS * a : PASS * (a + 1), PASS * b : PASS * (b + 1)].rearrange("(p j) c -> p j c", j=PACK),
+            )
+
+        def load_tab2(a, slot):
+            tab2_w[a] = staged("tab2_w%d" % a, slot, [P, T], U32)
+            load_words(tab2_w[a], tab2_words[a])
+
+        def load_wo(slot):
+            late["wo"] = staged("wo_w", slot, [P, 2 * N], U32)
+            nc.sync.dma_start(
+                out=late["wo"][:].bitcast(I32).rearrange("p (a c) -> p a c", a=2),
+                in_=wo_words.rearrange("a p c i -> p a (c i)").bitcast(I32),
+            )
+
+        def load_base(slot):
+            late["base"] = staged("base_t", slot, [P, N // P, M], F32)
+            nc.sync.dma_start(out=late["base"][:], in_=base.rearrange("(c p) m -> p c m", p=P))
+
+        v_sc_both = sb("v_sc_both", [P, S], U8)
+
+        def gather_tab_scales():
+            nc.vector.tensor_copy(v_sc_both[:], tab_sc[:].indirect(offs_t[:]))
+            for a in range(2):
+                shift = DEAD + 4 * a
+                nc.sync.dma_start(
+                    out=v_sc[a][0 : P - shift, :].bitcast(I32), in_=v_sc_both[shift:P, :].bitcast(I32)
+                )
+
+        wc_w = [sb("wc_w%d" % b, [P, 2 * PACK * 2 * P], U8) for b in range(2)]
+        wc_sc = [sb("wc_sc%d" % b, [P, 2 * PACK * P], U8) for b in range(2)]
+
+        def order_wc_scales(b):
+            nc.gpsimd.tensor_copy(
+                wc_sc[b][:].rearrange("p (a t m) -> p a t m", a=2, t=PACK),
+                wc_sc_raw[:].rearrange("p (a b m t) -> p b a t m", a=2, b=2, t=PACK)[:, b],
+            )
+
+        def order_wc_words(b):
+            for a in range(2):
+                nc.gpsimd.tensor_copy(
+                    wc_w[b][:].rearrange("p (a t m e) -> p a t m e", a=2, t=PACK, e=2)[:, a],
+                    wc_raw[:].rearrange("p (a b m t e) -> p a b t m e", a=2, b=2, t=PACK, e=2)[:, a, b],
+                )
+
+        v_w = {}
+
+        def gather_tab(a, h):
+            v_w[a, h] = sb("v_w%d%d" % (a, h), [P, BANK], U32)
+            nc.vector.tensor_copy(v_w[a, h][:], tab_w[a][:].indirect(offs_t[:, 32 * h : 32 * (h + 1)]))
+
+        coarse = [sb("coarse%d" % k, [P, S], F32) for k in range(2 * PACK)]
+
+        def coarse_half(b, t, h):
+            acc = psum.tile([P, BANK], F32, tag="wide", name="acc")
+            cols = slice(BANK * h, BANK * (h + 1))
+            for a in range(2):
+                slot = a * PACK + t
+                nc.tensor.matmul_mx(
+                    out=acc[:],
+                    lhsT=wc_w[b][:, 2 * P * slot : 2 * P * (slot + 1)].bitcast(FP4X4),
+                    lhsT_scale=wc_sc[b][:, P * slot : P * (slot + 1)],
+                    rhs=v_w[a, h][:].bitcast(FP8X4),
+                    rhs_scale=v_sc[a][:, cols],
+                    start=(a == 0),
+                    stop=(a == 1),
+                )
+            nc.scalar.activation(coarse[PACK * b + t][:, cols], acc[:], ACT.Copy)
+
+        wf_w, wf_sc, wf_bf = {}, {}, {}
+
+        def round_wf(copy, a, b):
+            if (a, b) == (1, 0):
+                wf_bf[a, b] = staged("wf_bf10", 7, [P, PACK * PASS], BF16)
+            else:
+                wf_bf[a, b] = sb("wf_bf%d%d" % (a, b), [P, PACK * PASS], BF16)
+            copy(
+                wf_bf[a, b][:].rearrange("p (t m j) -> p m j t", t=PACK, j=PACK),
+                wf_raw[a, b][:].rearrange("p j (m t) -> p m j t", t=PACK),
+            )
+
+        def quantize_wf(a, b):
+            wf_w[a, b] = sb("wf_w%d%d" % (a, b), [P, PASS], U32)
+            wf_sc[a, b] = sb("wf_sc%d%d" % (a, b), [P, PASS], U8)
+            nc.vector.quantize_mx(out=wf_w[a, b][:].bitcast(FP8X4), scales=wf_sc[a, b][:], in_=wf_bf[a, b][:])
+
+        v2_sc = sb("v2_sc", [P, M], U8)
+        v2_w = [sb("v2_w%d" % a, [P, M], U32) for a in range(2)]
+
+        def gather_tab2_scales():
+            nc.vector.tensor_copy(v2_sc[:], tab2_sc[:].indirect(offs2_t[:]))
+
+        def gather_tab2(a):
+            nc.vector.tensor_copy(v2_w[a][:], tab2_w[a][:].indirect(offs2_t[:]))
+
+        picked, scaled, fine, diff, step = {}, {}, {}, {}, {}
+
+        def pick(b, t):
+            if (b, t) == (1, PACK - 1):
+                picked[b, t] = staged("picked_last", 7, [P, M], F32)
+            else:
+                picked[b, t] = sb("picked%d%d" % (b, t), [P, M], F32)
+            nc.vector.tensor_copy(picked[b, t][:], coarse[PACK * b + t][:].indirect(pos_t[:]))
+
+        def scale_picked(b, t):
+            nc.gpsimd.tensor_scalar(
+                scaled[b][:, t, :], picked[b, t][:], level_t[:, b, t : t + 1], 0.0, ALU.mult, ALU.add
+            )
+
+        def fine_product(b, t):
+            fine[b, t] = psum.tile([P, M], F32, tag="fine", name="fine")
+            cols = slice(P * t, P * (t + 1))
+            for a in range(2):
+                nc.tensor.matmul_mx(
+                    out=fine[b, t][:],
+                    lhsT=wf_w[a, b][:, cols].bitcast(FP8X4),
+                    lhsT_scale=wf_sc[a, b][:, cols],
+                    rhs=v2_w[a][:].bitcast(FP8X4),
+                    rhs_scale=v2_sc[4 * a : P, :],
+                    start=(a == 0),
+                    stop=(a == 1),
+                )
+
+        def difference(b, t):
+            diff[b, t] = keep.tile([P, M], F32, name="diff", tag="diff", bufs=4)
+            nc.vector.tensor_tensor(diff[b, t][:], fine[b, t][:], picked[b, t][:], ALU.subtract)
+            step[b, t] = sb("step%d%d" % (b, t), [P, M], F32)
+            nc.scalar.activation(step[b, t][:], diff[b, t][:], ACT.Tanh)
+
+        z_rows = {}
+        for b in range(2):
+            for h in range(2):
+                z_rows[b, h] = sb("z_rows%d%d" % (b, h), [P, PACK, HALF], BF16)
+
+        def blend(b, h, t):
+            cols = slice(HALF * h, HALF * (h + 1))
+            nc.vector.scalar_tensor_tensor(
+                z_rows[b, h][:, t, :], step[b, t][:, cols], fade_t[:, b, t : t + 1], scaled[b][:, t, cols],
+                ALU.mult, ALU.add,
+            )
+
+        z_bf, z_w, z_sc = {}, {}, {}
+
+        def weave(b, h):
+            z_bf[b, h] = sb("z_bf%d%d" % (b, h), [P, HALF * PACK], BF16)
+            nc.scalar.copy(
+                z_bf[b, h][:].rearrange("p (c i t) -> p c t i", i=4, t=PACK),
+                z_rows[b, h][:].rearrange("p t (c i) -> p c t i", i=4),
+            )
+
+        def quantize_z(b, h):
+            z_w[b, h] = sb("z_w%d%d" % (b, h), [P, HALF], U32)
+            z_sc[b, h] = sb("z_sc%d%d" % (b, h), [P, HALF], U8)
+            nc.vector.quantize_mx(out=z_w[b, h][:].bitcast(FP8X4), scales=z_sc[b, h][:], in_=z_bf[b, h][:])
+
+        height = {}
+
+        def height_passes(b, h, pair):
+            if b == 0:
+                height[h, pair] = psum.tile([P, BANK], F32, tag="wide", name="height")
+            for i in range(2):
+                c = 2 * pair + i
+                nc.tensor.matmul_mx(
+                    out=height[h, pair][:, HALF * i : HALF * (i + 1)],
+                    lhsT=late["wo"][:, N * b + P * c : N * b + P * (c + 1)].bitcast(FP8X4),
+                    lhsT_scale=wo_sc[4 * b : P, P * c : P * (c + 1)],
+                    rhs=z_w[b, h][:].bitcast(FP8X4),
+                    rhs_scale=z_sc[b, h][:],
+                    start=(b == 0 and i == 0),
+                    stop=(b == 1 and i == 1),
+                )
+
+        def finish(h, pair):
+            acc = height[h, pair]
+            cols = slice(HALF * h, HALF * (h + 1))
+            result = sb("result%d%d" % (h, pair), [P, 2, HALF], F32)
+            nc.vector.tensor_tensor(
+                result[:], acc[:].rearrange("p (i m) -> p i m", i=2), late["base"][:, 2 * pair : 2 * pair + 2, cols], ALU.add
+            )
+            nc.sync.dma_start(
+                out=out[2 * P * pair : 2 * P * (pair + 1), cols].rearrange("(i p) m -> p i m", p=P), in_=result[:]
+            )
+
+        gather_tab_scales()
+        order_wc_words(0)
+        load_tab2(0, 2)
+        load_planes_packed(tab2_sc, 0, tab2_scales)
+        load_tab2(1, 3)
+        load_factors()
+        load_wf(0, 0, 4)
+        load_wf(1, 0, 5)
+        load_wf(0, 1, 6)
+        order_wc_scales(0)
+        order_wc_words(1)
+        order_wc_scales(1)
+        gather_tab(0, 0)
+        gather_tab(1, 0)
+        for t in range(PACK):
+            coarse_half(0, t, 0)
+        gather_tab(0, 1)
+        gather_tab(1, 1)
+        load_wf(1, 1, 0)
+        load_planes_packed(wo_sc, 0, wo_scales)
+        load_wo(1)
+        for t in range(PACK):
+            coarse_half(0, t, 1)
+        for t in range(PACK):
+            for h in range(2):
+                coarse_half(1, t, h)
+        gather_tab2(0)
+        load_base(2)
+        gather_tab2_scales()
+        gather_tab2(1)
+        for a in range(2):
+            round_wf(nc.scalar.copy, a, 0)
+            quantize_wf(a, 0)
+        for t in range(PACK):
+            fine_product(0, t)
+        for b in range(2):
+            for t in range(PACK):
+                pick(b, t)
+        scaled[0] = sb("scaled0", [P, PACK, M], F32)
+        scaled[1] = sb("scaled1", [P, PACK, M], F32)
+        for b in range(2):
+            for t in range(PACK):
+                scale_picked(b, t)
+        for a in range(2):
+            round_wf(nc.scalar.copy, a, 1)
+        for t in range(PACK):
+            difference(0, t)
+        for a in range(2):
+            quantize_wf(a, 1)
+        for t in range(PACK):
+            fine_product(1, t)
+        for h in range(2):
+            for t in range(PACK):
+                blend(0, h, t)
+            weave(0, h)
+        for t in range(PACK):
+            difference(1, t)
+        for h in range(2):
+            quantize_z(0, h)
+            for pair in range(2):
+                height_passes(0, h, pair)
+        for h in range(2):
+            for t in range(PACK):
+                blend(1, h, t)
+            weave(1, h)
+        for h in range(2):
+            quantize_z(1, h)
+            for pair in range(2):
+                height_passes(1, h, pair)
+        for h in range(2):
+            for pair in range(2):
+                finish(h, pair)

@@ -23,6 +23,7 @@ BANK = 512
 HALF = M // 2
 QUADS = 4
 DEAD = 24
+HELD = 2
 
 
 def tile_list_lunar_tile_morph_kernel(
@@ -62,19 +63,22 @@ def tile_list_lunar_tile_morph_kernel(
         tab2_sc = sb("tab2_sc", [P, T], U8)
         v_sc = [sb("v_sc%d" % a, [P, S], U8) for a in range(2)]
         wo_sc = sb("wo_sc", [P, N], U8)
-        zero(nc.vector, wc_sc_raw)
         for q in range(QUADS):
             zero(nc.vector, tab_sc[32 * q : 32 * q + DEAD, :])
-        for tile in (v_sc[0], v_sc[1], tab2_sc, wo_sc):
+        for tile in (wc_sc_raw, v_sc[0], v_sc[1], tab2_sc, wo_sc):
             zero(nc.gpsimd, tile)
 
         nc.sync.dma_start(offs_t[:], offs)
         load_planes_packed(tab_sc, DEAD, tab_scales)
-        wc_raw = sb("wc_raw", [P, 2 * 2 * H], U8)
-        nc.sync.dma_start(
-            out=wc_raw[:].bitcast(I32).rearrange("p (a c) -> p a c", a=2),
-            in_=wc_words.bitcast(I32).rearrange("a p c -> p a c"),
-        )
+        wc_raw = [sb("wc_raw%d" % b, [P, 2 * 2 * PASS], U8) for b in range(2)]
+
+        def load_wc(b):
+            nc.sync.dma_start(
+                out=wc_raw[b][:].bitcast(I32).rearrange("p (a c) -> p a c", a=2),
+                in_=wc_words[:, :, 2 * PASS * b : 2 * PASS * (b + 1)].bitcast(I32).rearrange("a p c -> p a c"),
+            )
+
+        load_wc(0)
         tab_w = [staged("tab_w%d" % a, a, [P, T], U32) for a in range(2)]
         load_words(tab_w[0], tab_words[0])
         nc.sync.dma_start(offs2_t[:], offs2)
@@ -116,7 +120,7 @@ def tile_list_lunar_tile_morph_kernel(
             late["base"] = staged("base_t", slot, [P, N // P, M], F32)
             nc.sync.dma_start(out=late["base"][:], in_=base.rearrange("(c p) m -> p c m", p=P))
 
-        v_sc_both = sb("v_sc_both", [P, S], U8)
+        v_sc_both = staged("v_sc_both", 8, [P, S], U8)
 
         def gather_tab_scales():
             nc.vector.tensor_copy(v_sc_both[:], tab_sc[:].indirect(offs_t[:]))
@@ -130,25 +134,28 @@ def tile_list_lunar_tile_morph_kernel(
         wc_sc = [sb("wc_sc%d" % b, [P, 2 * PACK * P], U8) for b in range(2)]
 
         def order_wc_scales(b):
-            nc.gpsimd.tensor_copy(
+            nc.vector.tensor_copy(
                 wc_sc[b][:].rearrange("p (a t m) -> p a t m", a=2, t=PACK),
                 wc_sc_raw[:].rearrange("p (a b m t) -> p b a t m", a=2, b=2, t=PACK)[:, b],
             )
 
         def order_wc_words(b):
-            for a in range(2):
-                nc.gpsimd.tensor_copy(
-                    wc_w[b][:].rearrange("p (a t m e) -> p a t m e", a=2, t=PACK, e=2)[:, a],
-                    wc_raw[:].rearrange("p (a b m t e) -> p a b t m e", a=2, b=2, t=PACK, e=2)[:, a, b],
-                )
+            nc.vector.tensor_copy(
+                wc_w[b][:].bitcast(U16).rearrange("p (a t m) -> p a t m", a=2, t=PACK),
+                wc_raw[b][:].bitcast(U16).rearrange("p (a m t) -> p a t m", a=2, t=PACK),
+            )
 
         v_w = {}
 
         def gather_tab(a, h):
-            v_w[a, h] = sb("v_w%d%d" % (a, h), [P, BANK], U32)
+            if (a, h) == (0, 1):
+                v_w[a, h] = staged("v_w01", 8, [P, BANK], U32)
+            else:
+                v_w[a, h] = sb("v_w%d%d" % (a, h), [P, BANK], U32)
             nc.vector.tensor_copy(v_w[a, h][:], tab_w[a][:].indirect(offs_t[:, 32 * h : 32 * (h + 1)]))
 
-        coarse = [sb("coarse%d" % k, [P, S], F32) for k in range(2 * PACK)]
+        coarse = [sb("coarse%d" % k, [P, S], F32) for k in range(2 * PACK - 1)]
+        coarse.append(staged("coarse_last", 9, [P, S], F32))
 
         def coarse_half(b, t, h):
             acc = psum.tile([P, BANK], F32, tag="wide", name="acc")
@@ -168,20 +175,21 @@ def tile_list_lunar_tile_morph_kernel(
 
         wf_w, wf_sc, wf_bf = {}, {}, {}
 
-        def round_wf(copy, a, b):
-            if (a, b) == (1, 0):
-                wf_bf[a, b] = staged("wf_bf10", 7, [P, PACK * PASS], BF16)
+        def round_wf(b):
+            if b == 0:
+                wf_bf[b] = staged("wf_bf0", 7, [P, 2 * PACK * PASS], BF16)
             else:
-                wf_bf[a, b] = sb("wf_bf%d%d" % (a, b), [P, PACK * PASS], BF16)
-            copy(
-                wf_bf[a, b][:].rearrange("p (t m j) -> p m j t", t=PACK, j=PACK),
-                wf_raw[a, b][:].rearrange("p j (m t) -> p m j t", t=PACK),
-            )
+                wf_bf[b] = sb("wf_bf1", [P, 2 * PACK * PASS], BF16)
+            for a in range(2):
+                nc.scalar.copy(
+                    wf_bf[b][:].rearrange("p (a t m j) -> p a m j t", a=2, t=PACK, j=PACK)[:, a],
+                    wf_raw[a, b][:].rearrange("p j (m t) -> p m j t", t=PACK),
+                )
 
-        def quantize_wf(a, b):
-            wf_w[a, b] = sb("wf_w%d%d" % (a, b), [P, PASS], U32)
-            wf_sc[a, b] = sb("wf_sc%d%d" % (a, b), [P, PASS], U8)
-            nc.vector.quantize_mx(out=wf_w[a, b][:].bitcast(FP8X4), scales=wf_sc[a, b][:], in_=wf_bf[a, b][:])
+        def quantize_wf(b):
+            wf_w[b] = sb("wf_w%d" % b, [P, 2 * PASS], U32)
+            wf_sc[b] = sb("wf_sc%d" % b, [P, 2 * PASS], U8)
+            nc.vector.quantize_mx(out=wf_w[b][:].bitcast(FP8X4), scales=wf_sc[b][:], in_=wf_bf[b][:])
 
         v2_sc = sb("v2_sc", [P, M], U8)
         v2_w = [sb("v2_w%d" % a, [P, M], U32) for a in range(2)]
@@ -195,8 +203,10 @@ def tile_list_lunar_tile_morph_kernel(
         picked, scaled, fine, diff, step = {}, {}, {}, {}, {}
 
         def pick(b, t):
-            if (b, t) == (1, PACK - 1):
-                picked[b, t] = staged("picked_last", 7, [P, M], F32)
+            if b == 1 and t >= PACK - HELD:
+                if t == PACK - HELD:
+                    late["picks"] = staged("picked_held", 7, [P, HELD * M], F32)
+                picked[b, t] = late["picks"][:, M * (t - PACK + HELD) : M * (t - PACK + HELD + 1)]
             else:
                 picked[b, t] = sb("picked%d%d" % (b, t), [P, M], F32)
             nc.vector.tensor_copy(picked[b, t][:], coarse[PACK * b + t][:].indirect(pos_t[:]))
@@ -208,12 +218,12 @@ def tile_list_lunar_tile_morph_kernel(
 
         def fine_product(b, t):
             fine[b, t] = psum.tile([P, M], F32, tag="fine", name="fine")
-            cols = slice(P * t, P * (t + 1))
             for a in range(2):
+                cols = slice(PASS * a + P * t, PASS * a + P * (t + 1))
                 nc.tensor.matmul_mx(
                     out=fine[b, t][:],
-                    lhsT=wf_w[a, b][:, cols].bitcast(FP8X4),
-                    lhsT_scale=wf_sc[a, b][:, cols],
+                    lhsT=wf_w[b][:, cols].bitcast(FP8X4),
+                    lhsT_scale=wf_sc[b][:, cols],
                     rhs=v2_w[a][:].bitcast(FP8X4),
                     rhs_scale=v2_sc[4 * a : P, :],
                     start=(a == 0),
@@ -240,9 +250,9 @@ def tile_list_lunar_tile_morph_kernel(
 
         z_bf, z_w, z_sc = {}, {}, {}
 
-        def weave(b, h):
+        def weave(copy, b, h):
             z_bf[b, h] = sb("z_bf%d%d" % (b, h), [P, HALF * PACK], BF16)
-            nc.scalar.copy(
+            copy(
                 z_bf[b, h][:].rearrange("p (c i t) -> p c t i", i=4, t=PACK),
                 z_rows[b, h][:].rearrange("p t (c i) -> p c t i", i=4),
             )
@@ -282,6 +292,7 @@ def tile_list_lunar_tile_morph_kernel(
 
         gather_tab_scales()
         order_wc_words(0)
+        load_wc(1)
         load_tab2(0, 2)
         load_planes_packed(tab2_sc, 0, tab2_scales)
         load_tab2(1, 3)
@@ -289,10 +300,8 @@ def tile_list_lunar_tile_morph_kernel(
         load_wf(0, 0, 4)
         load_wf(1, 0, 5)
         load_wf(0, 1, 6)
-        order_wc_scales(0)
-        order_wc_words(1)
-        order_wc_scales(1)
         gather_tab(0, 0)
+        order_wc_scales(0)
         gather_tab(1, 0)
         for t in range(PACK):
             coarse_half(0, t, 0)
@@ -303,40 +312,41 @@ def tile_list_lunar_tile_morph_kernel(
         load_wo(1)
         for t in range(PACK):
             coarse_half(0, t, 1)
-        for t in range(PACK):
+        order_wc_words(1)
+        order_wc_scales(1)
+        for t in range(PACK - HELD):
             for h in range(2):
                 coarse_half(1, t, h)
         gather_tab2(0)
         load_base(2)
         gather_tab2_scales()
         gather_tab2(1)
-        for a in range(2):
-            round_wf(nc.scalar.copy, a, 0)
-            quantize_wf(a, 0)
+        round_wf(0)
+        for t in range(PACK - HELD, PACK):
+            for h in range(2):
+                coarse_half(1, t, h)
+        quantize_wf(0)
         for t in range(PACK):
             fine_product(0, t)
         for b in range(2):
             for t in range(PACK):
                 pick(b, t)
-        scaled[0] = sb("scaled0", [P, PACK, M], F32)
-        scaled[1] = sb("scaled1", [P, PACK, M], F32)
-        for b in range(2):
-            for t in range(PACK):
-                scale_picked(b, t)
-        for a in range(2):
-            round_wf(nc.scalar.copy, a, 1)
+        round_wf(1)
+        scaled[0] = staged("scaled0", 9, [P, PACK, M], F32)
         for t in range(PACK):
             difference(0, t)
-        for a in range(2):
-            quantize_wf(a, 1)
+            scale_picked(0, t)
+        quantize_wf(1)
         for t in range(PACK):
             fine_product(1, t)
         for h in range(2):
             for t in range(PACK):
                 blend(0, h, t)
-            weave(0, h)
+            weave(nc.scalar.copy, 0, h)
+        scaled[1] = staged("scaled1", 9, [P, PACK, M], F32)
         for t in range(PACK):
             difference(1, t)
+            scale_picked(1, t)
         for h in range(2):
             quantize_z(0, h)
             for pair in range(2):
@@ -344,11 +354,11 @@ def tile_list_lunar_tile_morph_kernel(
         for h in range(2):
             for t in range(PACK):
                 blend(1, h, t)
-            weave(1, h)
+        weave(nc.scalar.copy, 1, 0)
+        quantize_z(1, 0)
+        weave(nc.vector.tensor_copy, 1, 1)
+        quantize_z(1, 1)
         for h in range(2):
-            quantize_z(1, h)
             for pair in range(2):
                 height_passes(1, h, pair)
-        for h in range(2):
-            for pair in range(2):
                 finish(h, pair)

@@ -181,10 +181,11 @@ def tile_list_lunar_tile_morph_kernel(
             else:
                 wf_bf[b] = sb("wf_bf1", [P, 2 * PACK * PASS], BF16)
             for a in range(2):
-                nc.scalar.copy(
-                    wf_bf[b][:].rearrange("p (a t m j) -> p a m j t", a=2, t=PACK, j=PACK)[:, a],
-                    wf_raw[a, b][:].rearrange("p j (m t) -> p m j t", t=PACK),
-                )
+                for u in range(2):
+                    nc.scalar.copy(
+                        wf_bf[b][:].rearrange("p (a u e m j) -> p a u m j e", a=2, u=2, e=2, j=PACK)[:, a, u],
+                        wf_raw[a, b][:].rearrange("p j (m u e) -> p u m j e", u=2, e=2)[:, u],
+                    )
 
         def quantize_wf(b):
             wf_w[b] = sb("wf_w%d" % b, [P, 2 * PASS], U32)
@@ -295,10 +296,9 @@ def tile_list_lunar_tile_morph_kernel(
         load_wc(1)
         load_tab2(0, 2)
         load_planes_packed(tab2_sc, 0, tab2_scales)
-        load_tab2(1, 3)
-        load_factors()
         load_wf(0, 0, 4)
         load_wf(1, 0, 5)
+        load_tab2(1, 3)
         load_wf(0, 1, 6)
         gather_tab(0, 0)
         order_wc_scales(0)
@@ -308,6 +308,7 @@ def tile_list_lunar_tile_morph_kernel(
         gather_tab(0, 1)
         gather_tab(1, 1)
         load_wf(1, 1, 0)
+        load_factors()
         load_planes_packed(wo_sc, 0, wo_scales)
         load_wo(1)
         for t in range(PACK):

@@ -22,8 +22,8 @@ PASS = P * PACK
 BANK = 512
 HALF = M // 2
 QUADS = 4
-DEAD = 24
-HELD = 2
+SLICES = H // P
+LIVE = 32 * (QUADS - 1) + 4
 
 
 def tile_list_lunar_tile_morph_kernel(
@@ -33,21 +33,23 @@ def tile_list_lunar_tile_morph_kernel(
     nc = tc.nc
     with ExitStack() as ctx:
         keep = ctx.enter_context(tc.tile_pool(name="keep", bufs=1))
-        psum = ctx.enter_context(tc.psum_pool(name="psum", bufs=4))
+        psum = ctx.enter_context(tc.psum_pool(name="psum", bufs=1))
 
-        def sb(name, shape, dtype):
-            return keep.tile(shape, dtype, name=name, align_bytes=64)
+        def sb(name, shape, dtype, slot=None):
+            if slot is None:
+                return keep.tile(shape, dtype, name=name, align_bytes=64)
+            return keep.tile(shape, dtype, name=name, tag=slot, bufs=1, align_bytes=64)
 
-        def staged(name, slot, shape, dtype):
-            return keep.tile(shape, dtype, name=name, tag="stage%d" % slot, bufs=1, align_bytes=64)
+        def bank(i, name, shape):
+            return psum.tile(shape, F32, name=name, tag="bank%d" % i, bufs=1)
 
         def zero(engine, tile):
             engine.memset(tile[:].bitcast(I32), 0)
 
-        def load_planes_packed(tile, first, scales):
+        def load_planes_packed(queue, tile, scales):
             for q in range(QUADS):
-                nc.sync.dma_start(
-                    out=tile[32 * q + first : 32 * q + first + 8, :].bitcast(I32),
+                queue.dma_start(
+                    out=tile[32 * q : 32 * q + 8, :].bitcast(I32),
                     in_=scales[:, 4 * q : 4 * q + 4, :].bitcast(I32),
                 )
 
@@ -58,19 +60,19 @@ def tile_list_lunar_tile_morph_kernel(
         pos_t = keep.tile([P, M // 16], U16, name="pos_t")
         offs2_t = keep.tile([P, M // 16], U16, name="offs2_t")
 
-        tab_sc = sb("tab_sc", [P, T], U8)
-        wc_sc_raw = sb("wc_sc_raw", [P, 2 * H], U8)
-        tab2_sc = sb("tab2_sc", [P, T], U8)
+        tab_sc = sb("tab_sc", [P, T], U8, "tab_sc")
+        wc_sc_raw = sb("wc_sc_raw", [P, 2 * H], U8, "wc_sc_raw")
+        tab2_sc = sb("tab2_sc", [P, T], U8, "tab2_sc")
         v_sc = [sb("v_sc%d" % a, [P, S], U8) for a in range(2)]
         wo_sc = sb("wo_sc", [P, N], U8)
-        for q in range(QUADS):
-            zero(nc.vector, tab_sc[32 * q : 32 * q + DEAD, :])
-        for tile in (wc_sc_raw, v_sc[0], v_sc[1], tab2_sc, wo_sc):
-            zero(nc.gpsimd, tile)
+        zero(nc.gpsimd, tab_sc)
+        for tile in (wc_sc_raw, tab2_sc, v_sc[1], wo_sc):
+            zero(nc.vector, tile)
 
         nc.sync.dma_start(offs_t[:], offs)
-        load_planes_packed(tab_sc, DEAD, tab_scales)
-        wc_raw = [sb("wc_raw%d" % b, [P, 2 * 2 * PASS], U8) for b in range(2)]
+        nc.sync.dma_start(pos_t[:], pos1)
+        load_planes_packed(nc.sync, tab_sc, tab_scales)
+        wc_raw = [sb("wc_raw%d" % b, [P, 2 * 2 * PASS], U8, "wc_raw%d" % b) for b in range(2)]
 
         def load_wc(b):
             nc.sync.dma_start(
@@ -78,17 +80,24 @@ def tile_list_lunar_tile_morph_kernel(
                 in_=wc_words[:, :, 2 * PASS * b : 2 * PASS * (b + 1)].bitcast(I32).rearrange("a p c -> p a c"),
             )
 
-        load_wc(0)
-        tab_w = [staged("tab_w%d" % a, a, [P, T], U32) for a in range(2)]
-        load_words(tab_w[0], tab_words[0])
-        nc.sync.dma_start(offs2_t[:], offs2)
-        for q in range(QUADS):
+        def load_wc_scales(queue):
+            for q in range(QUADS):
+                queue.dma_start(
+                    out=wc_sc_raw[32 * q : 32 * q + 4, :].bitcast(I32).rearrange("r (a c) -> r a c", a=2),
+                    in_=wc_scales[:, 4 * q : 4 * q + 4, :].bitcast(I32).rearrange("a r c -> r a c"),
+                )
+
+        wf_raw = {}
+
+        def load_wf(a, b):
+            wf_raw[a, b] = sb("wf_raw%d%d" % (a, b), [P, PACK, PASS], F32, "wf%d%d" % (a, b))
             nc.sync.dma_start(
-                out=wc_sc_raw[32 * q : 32 * q + 4, :].bitcast(I32).rearrange("r (a c) -> r a c", a=2),
-                in_=wc_scales[:, 4 * q : 4 * q + 4, :].bitcast(I32).rearrange("a r c -> r a c"),
+                out=wf_raw[a, b][:],
+                in_=wf[PASS * a : PASS * (a + 1), PASS * b : PASS * (b + 1)].rearrange("(p j) c -> p j c", j=PACK),
             )
-        load_words(tab_w[1], tab_words[1])
-        nc.sync.dma_start(pos_t[:], pos1)
+
+        tab_w = [sb("tab_w%d" % a, [P, T], U32, "tab%d" % a) for a in range(2)]
+        tab2_w = [sb("tab2_w%d" % a, [P, T], U32, "tab2%d" % a) for a in range(2)]
         level_t = sb("level_t", [P, 2, PACK], F32)
         fade_t = sb("fade_t", [P, 2, PACK], F32)
 
@@ -96,44 +105,43 @@ def tile_list_lunar_tile_morph_kernel(
             nc.sync.dma_start(out=level_t[:], in_=level.rearrange("(b p t) -> p b t", b=2, t=PACK))
             nc.sync.dma_start(out=fade_t[:], in_=fade.rearrange("(b p t) -> p b t", b=2, t=PACK))
 
-        wf_raw, tab2_w, late = {}, {}, {}
+        def gather_tab_scales():
+            nc.vector.tensor_copy(v_sc[0][:], tab_sc[:].indirect(offs_t[:]))
+            nc.sync.dma_start(out=v_sc[1][0:LIVE, :].bitcast(I32), in_=v_sc[0][4 : 4 + LIVE, :].bitcast(I32))
 
-        def load_wf(a, b, slot):
-            wf_raw[a, b] = staged("wf_raw%d%d" % (a, b), slot, [P, PACK, PASS], F32)
-            nc.sync.dma_start(
-                out=wf_raw[a, b][:],
-                in_=wf[PASS * a : PASS * (a + 1), PASS * b : PASS * (b + 1)].rearrange("(p j) c -> p j c", j=PACK),
-            )
+        load_wc(0)
+        load_words(tab_w[0], tab_words[0])
+        load_wc_scales(nc.sync)
+        load_words(tab_w[1], tab_words[1])
+        gather_tab_scales()
+        load_wc(1)
+        load_words(tab2_w[0], tab2_words[0])
+        nc.sync.dma_start(offs2_t[:], offs2)
+        load_wf(0, 0)
+        load_planes_packed(nc.sync, tab2_sc, tab2_scales)
+        load_wf(1, 0)
+        load_factors()
+        load_words(tab2_w[1], tab2_words[1])
+        load_wf(0, 1)
+        load_wf(1, 1)
 
-        def load_tab2(a, slot):
-            tab2_w[a] = staged("tab2_w%d" % a, slot, [P, T], U32)
-            load_words(tab2_w[a], tab2_words[a])
+        late = {}
 
-        def load_wo(slot):
-            late["wo"] = staged("wo_w", slot, [P, 2 * N], U32)
+        def load_late():
+            load_planes_packed(nc.sync, wo_sc, wo_scales)
+            late["wo"] = sb("wo_w", [P, 2 * N], U32, "tab1")
             nc.sync.dma_start(
                 out=late["wo"][:].bitcast(I32).rearrange("p (a c) -> p a c", a=2),
                 in_=wo_words.rearrange("a p c i -> p a (c i)").bitcast(I32),
             )
-
-        def load_base(slot):
-            late["base"] = staged("base_t", slot, [P, N // P, M], F32)
+            late["base"] = sb("base_t", [P, N // P, M], F32, "tab0")
             nc.sync.dma_start(out=late["base"][:], in_=base.rearrange("(c p) m -> p c m", p=P))
 
-        v_sc_both = staged("v_sc_both", 8, [P, S], U8)
-
-        def gather_tab_scales():
-            nc.vector.tensor_copy(v_sc_both[:], tab_sc[:].indirect(offs_t[:]))
-            for a in range(2):
-                shift = DEAD + 4 * a
-                nc.sync.dma_start(
-                    out=v_sc[a][0 : P - shift, :].bitcast(I32), in_=v_sc_both[shift:P, :].bitcast(I32)
-                )
-
         wc_w = [sb("wc_w%d" % b, [P, 2 * PACK * 2 * P], U8) for b in range(2)]
-        wc_sc = [sb("wc_sc%d" % b, [P, 2 * PACK * P], U8) for b in range(2)]
+        wc_sc = {}
 
-        def order_wc_scales(b):
+        def order_wc_scales(b, slot=None):
+            wc_sc[b] = sb("wc_sc%d" % b, [P, 2 * PACK * P], U8, slot)
             nc.vector.tensor_copy(
                 wc_sc[b][:].rearrange("p (a t m) -> p a t m", a=2, t=PACK),
                 wc_sc_raw[:].rearrange("p (a b m t) -> p b a t m", a=2, b=2, t=PACK)[:, b],
@@ -147,48 +155,49 @@ def tile_list_lunar_tile_morph_kernel(
 
         v_w = {}
 
-        def gather_tab(a, h):
-            if (a, h) == (0, 1):
-                v_w[a, h] = staged("v_w01", 8, [P, BANK], U32)
-            else:
-                v_w[a, h] = sb("v_w%d%d" % (a, h), [P, BANK], U32)
+        def gather_tab(a, h, slot=None):
+            v_w[a, h] = sb("v_w%d%d" % (a, h), [P, BANK], U32, slot)
             nc.vector.tensor_copy(v_w[a, h][:], tab_w[a][:].indirect(offs_t[:, 32 * h : 32 * (h + 1)]))
 
-        coarse = [sb("coarse%d" % k, [P, S], F32) for k in range(2 * PACK - 1)]
-        coarse.append(staged("coarse_last", 9, [P, S], F32))
+        coarse = [sb("coarse%d" % k, [P, S], F32, "coarse%d" % k) for k in range(SLICES)]
 
-        def coarse_half(b, t, h):
-            acc = psum.tile([P, BANK], F32, tag="wide", name="acc")
+        def coarse_half(k, h):
+            b, t = divmod(k, PACK)
+            acc = bank((2 * k + h) % 4, "acc", [P, BANK])
             cols = slice(BANK * h, BANK * (h + 1))
             for a in range(2):
-                slot = a * PACK + t
+                place = a * PACK + t
                 nc.tensor.matmul_mx(
                     out=acc[:],
-                    lhsT=wc_w[b][:, 2 * P * slot : 2 * P * (slot + 1)].bitcast(FP4X4),
-                    lhsT_scale=wc_sc[b][:, P * slot : P * (slot + 1)],
+                    lhsT=wc_w[b][:, 2 * P * place : 2 * P * (place + 1)].bitcast(FP4X4),
+                    lhsT_scale=wc_sc[b][:, P * place : P * (place + 1)],
                     rhs=v_w[a, h][:].bitcast(FP8X4),
                     rhs_scale=v_sc[a][:, cols],
                     start=(a == 0),
                     stop=(a == 1),
                 )
-            nc.scalar.activation(coarse[PACK * b + t][:, cols], acc[:], ACT.Copy)
+            nc.scalar.activation(coarse[k][:, cols], acc[:], ACT.Copy)
 
-        wf_w, wf_sc, wf_bf = {}, {}, {}
+        wf_w, wf_sc = {}, {}
+        wf_bf = [sb("wf_bf%d" % b, [P, 2 * PACK * PASS], BF16, "wf_bf%d" % b) for b in range(2)]
 
-        def round_wf(b):
-            if b == 0:
-                wf_bf[b] = staged("wf_bf0", 7, [P, 2 * PACK * PASS], BF16)
-            else:
-                wf_bf[b] = sb("wf_bf1", [P, 2 * PACK * PASS], BF16)
-            for a in range(2):
-                for u in range(2):
-                    nc.scalar.copy(
-                        wf_bf[b][:].rearrange("p (a u e m j) -> p a u m j e", a=2, u=2, e=2, j=PACK)[:, a, u],
-                        wf_raw[a, b][:].rearrange("p j (m u e) -> p u m j e", u=2, e=2)[:, u],
-                    )
+        def round_wf_scalar(a, b):
+            for u in range(2):
+                nc.scalar.copy(
+                    wf_bf[b][:].rearrange("p (a u e m j) -> p a u m j e", a=2, u=2, e=2, j=PACK)[:, a, u],
+                    wf_raw[a, b][:].rearrange("p j (m u e) -> p u m j e", u=2, e=2)[:, u],
+                )
 
-        def quantize_wf(b):
-            wf_w[b] = sb("wf_w%d" % b, [P, 2 * PASS], U32)
+        def round_wf_gpsimd(a, b):
+            for t in range(0, PACK, 2):
+                nc.gpsimd.tensor_scalar(
+                    wf_bf[b][:].rearrange("p (a t m j) -> p a t m j", a=2, t=PACK, j=PACK)[:, a, t : t + 2],
+                    wf_raw[a, b][:].rearrange("p j (m t) -> p t m j", t=PACK)[:, t : t + 2],
+                    1.0, 0.0, ALU.mult, ALU.add,
+                )
+
+        def quantize_wf(b, slot):
+            wf_w[b] = sb("wf_w%d" % b, [P, 2 * PASS], U32, slot)
             wf_sc[b] = sb("wf_sc%d" % b, [P, 2 * PASS], U8)
             nc.vector.quantize_mx(out=wf_w[b][:].bitcast(FP8X4), scales=wf_sc[b][:], in_=wf_bf[b][:])
 
@@ -201,165 +210,163 @@ def tile_list_lunar_tile_morph_kernel(
         def gather_tab2(a):
             nc.vector.tensor_copy(v2_w[a][:], tab2_w[a][:].indirect(offs2_t[:]))
 
-        picked, scaled, fine, diff, step = {}, {}, {}, {}, {}
+        picked, scaled, fine, step = {}, {}, {}, {}
 
-        def pick(b, t):
-            if b == 1 and t >= PACK - HELD:
-                if t == PACK - HELD:
-                    late["picks"] = staged("picked_held", 7, [P, HELD * M], F32)
-                picked[b, t] = late["picks"][:, M * (t - PACK + HELD) : M * (t - PACK + HELD + 1)]
-            else:
-                picked[b, t] = sb("picked%d%d" % (b, t), [P, M], F32)
-            nc.vector.tensor_copy(picked[b, t][:], coarse[PACK * b + t][:].indirect(pos_t[:]))
+        def pick(k, slot=None):
+            if k // 2 not in picked:
+                picked[k // 2] = sb("picked%d" % k, [P, 2, M], F32, slot)
+            nc.vector.tensor_copy(picked[k // 2][:, k % 2, :], coarse[k][:].indirect(pos_t[:]))
 
-        def scale_picked(b, t):
+        def scale_pick(k, slot=None):
+            b, t = divmod(k, PACK)
+            if b not in scaled:
+                scaled[b] = sb("scaled%d" % b, [P, PACK, M], F32, slot)
             nc.gpsimd.tensor_scalar(
-                scaled[b][:, t, :], picked[b, t][:], level_t[:, b, t : t + 1], 0.0, ALU.mult, ALU.add
+                scaled[b][:, t, :], picked[k // 2][:, k % 2, :], level_t[:, b, t : t + 1], 0.0, ALU.mult, ALU.add
             )
 
-        def fine_product(b, t):
-            fine[b, t] = psum.tile([P, M], F32, tag="fine", name="fine")
-            for a in range(2):
-                cols = slice(PASS * a + P * t, PASS * a + P * (t + 1))
-                nc.tensor.matmul_mx(
-                    out=fine[b, t][:],
-                    lhsT=wf_w[b][:, cols].bitcast(FP8X4),
-                    lhsT_scale=wf_sc[b][:, cols],
-                    rhs=v2_w[a][:].bitcast(FP8X4),
-                    rhs_scale=v2_sc[4 * a : P, :],
-                    start=(a == 0),
-                    stop=(a == 1),
+        def fine_product(g, h, i):
+            fine[g, h] = bank(i, "fine", [P, 2, HALF])
+            cols_m = slice(HALF * h, HALF * (h + 1))
+            for e in range(2):
+                b, t = divmod(2 * g + e, PACK)
+                for a in range(2):
+                    cols = slice(PASS * a + P * t, PASS * a + P * (t + 1))
+                    nc.tensor.matmul_mx(
+                        out=fine[g, h][:, e, :],
+                        lhsT=wf_w[b][:, cols].bitcast(FP8X4),
+                        lhsT_scale=wf_sc[b][:, cols],
+                        rhs=v2_w[a][:, cols_m].bitcast(FP8X4),
+                        rhs_scale=v2_sc[4 * a : P, cols_m],
+                        start=(a == 0),
+                        stop=(a == 1),
+                    )
+
+        diffs = {}
+
+        def difference(g, h, slot=None, step_slot=None):
+            if g // 2 not in diffs:
+                diffs[g // 2] = sb("diff%d" % (g // 2), [P, 2, 2, M // 2 * 2], F32, slot)
+            diff = diffs[g // 2][:, h, g % 2, :].rearrange("p (e m) -> p e m", e=2)
+            nc.vector.tensor_tensor(diff[:], fine[g, h][:], picked[g][:, :, HALF * h : HALF * (h + 1)], ALU.subtract)
+            step[g, h] = sb("step%d%d" % (g, h), [P, 2, HALF], F32, step_slot)
+            nc.scalar.activation(step[g, h][:], diff[:], ACT.Tanh)
+
+        z_rows, z_bf, z_w, z_sc = {}, {}, {}, {}
+
+        def blend(b, m0, n, slot=None):
+            z_rows[b, m0] = sb("z_rows%d%d" % (b, m0), [P, PACK, n * P], BF16, slot)
+            h, within = divmod(P * m0, HALF)
+            for t in range(PACK):
+                nc.vector.scalar_tensor_tensor(
+                    z_rows[b, m0][:, t, :], step[2 * b + t // 2, h][:, t % 2, within : within + n * P], fade_t[:, b, t : t + 1],
+                    scaled[b][:, t, P * m0 : P * (m0 + n)], ALU.mult, ALU.add,
                 )
 
-        def difference(b, t):
-            diff[b, t] = keep.tile([P, M], F32, name="diff", tag="diff", bufs=4)
-            nc.vector.tensor_tensor(diff[b, t][:], fine[b, t][:], picked[b, t][:], ALU.subtract)
-            step[b, t] = sb("step%d%d" % (b, t), [P, M], F32)
-            nc.scalar.activation(step[b, t][:], diff[b, t][:], ACT.Tanh)
-
-        z_rows = {}
-        for b in range(2):
-            for h in range(2):
-                z_rows[b, h] = sb("z_rows%d%d" % (b, h), [P, PACK, HALF], BF16)
-
-        def blend(b, h, t):
-            cols = slice(HALF * h, HALF * (h + 1))
-            nc.vector.scalar_tensor_tensor(
-                z_rows[b, h][:, t, :], step[b, t][:, cols], fade_t[:, b, t : t + 1], scaled[b][:, t, cols],
-                ALU.mult, ALU.add,
-            )
-
-        z_bf, z_w, z_sc = {}, {}, {}
-
-        def weave(copy, b, h):
-            z_bf[b, h] = sb("z_bf%d%d" % (b, h), [P, HALF * PACK], BF16)
+        def weave(copy, b, m0, n, slot=None):
+            z_bf[b, m0] = sb("z_bf%d%d" % (b, m0), [P, n * P * PACK], BF16, slot)
             copy(
-                z_bf[b, h][:].rearrange("p (c i t) -> p c t i", i=4, t=PACK),
-                z_rows[b, h][:].rearrange("p t (c i) -> p c t i", i=4),
+                z_bf[b, m0][:].rearrange("p (c i t) -> p c t i", i=4, t=PACK),
+                z_rows[b, m0][:].rearrange("p t (c i) -> p c t i", i=4),
             )
 
-        def quantize_z(b, h):
-            z_w[b, h] = sb("z_w%d%d" % (b, h), [P, HALF], U32)
-            z_sc[b, h] = sb("z_sc%d%d" % (b, h), [P, HALF], U8)
-            nc.vector.quantize_mx(out=z_w[b, h][:].bitcast(FP8X4), scales=z_sc[b, h][:], in_=z_bf[b, h][:])
+        def quantize_z(b, m0, n, slot=None):
+            z_w[b, m0] = sb("z_w%d%d" % (b, m0), [P, n * P], U32, slot)
+            z_sc[b, m0] = sb("z_sc%d%d" % (b, m0), [P, n * P], U8)
+            nc.vector.quantize_mx(out=z_w[b, m0][:].bitcast(FP8X4), scales=z_sc[b, m0][:], in_=z_bf[b, m0][:])
 
         height = {}
 
-        def height_passes(b, h, pair):
-            if b == 0:
-                height[h, pair] = psum.tile([P, BANK], F32, tag="wide", name="height")
-            for i in range(2):
-                c = 2 * pair + i
+        def height_passes(b, m0, n, banks):
+            per = BANK // (n * P)
+            for c in range(N // P):
+                if b == 0 and c % per == 0:
+                    height[m0, c // per] = bank(banks[c // per], "height", [P, per, n * P])
                 nc.tensor.matmul_mx(
-                    out=height[h, pair][:, HALF * i : HALF * (i + 1)],
+                    out=height[m0, c // per][:, c % per, :],
                     lhsT=late["wo"][:, N * b + P * c : N * b + P * (c + 1)].bitcast(FP8X4),
                     lhsT_scale=wo_sc[4 * b : P, P * c : P * (c + 1)],
-                    rhs=z_w[b, h][:].bitcast(FP8X4),
-                    rhs_scale=z_sc[b, h][:],
-                    start=(b == 0 and i == 0),
-                    stop=(b == 1 and i == 1),
+                    rhs=z_w[b, m0][:].bitcast(FP8X4),
+                    rhs_scale=z_sc[b, m0][:],
+                    start=(b == 0 and c % per == 0),
+                    stop=(b == 1 and c % per == per - 1),
                 )
 
-        def finish(h, pair):
-            acc = height[h, pair]
-            cols = slice(HALF * h, HALF * (h + 1))
-            result = sb("result%d%d" % (h, pair), [P, 2, HALF], F32)
-            nc.vector.tensor_tensor(
-                result[:], acc[:].rearrange("p (i m) -> p i m", i=2), late["base"][:, 2 * pair : 2 * pair + 2, cols], ALU.add
-            )
+        def finish(m0, n, i, slot=None):
+            per = BANK // (n * P)
+            cols = slice(P * m0, P * (m0 + n))
+            result = sb("result%d%d" % (m0, i), [P, per, n * P], F32, slot)
+            nc.vector.tensor_tensor(result[:], height[m0, i][:], late["base"][:, per * i : per * (i + 1), cols], ALU.add)
             nc.sync.dma_start(
-                out=out[2 * P * pair : 2 * P * (pair + 1), cols].rearrange("(i p) m -> p i m", p=P), in_=result[:]
+                out=out[per * P * i : per * P * (i + 1), cols].rearrange("(i p) m -> p i m", p=P), in_=result[:]
             )
 
-        gather_tab_scales()
         order_wc_words(0)
-        load_wc(1)
-        load_tab2(0, 2)
-        load_planes_packed(tab2_sc, 0, tab2_scales)
-        load_wf(0, 0, 4)
-        load_wf(1, 0, 5)
-        load_tab2(1, 3)
-        load_wf(0, 1, 6)
         gather_tab(0, 0)
+        gather_tab(0, 1)
         order_wc_scales(0)
         gather_tab(1, 0)
-        for t in range(PACK):
-            coarse_half(0, t, 0)
-        gather_tab(0, 1)
+        coarse_half(0, 0)
         gather_tab(1, 1)
-        load_wf(1, 1, 0)
-        load_factors()
-        load_planes_packed(wo_sc, 0, wo_scales)
-        load_wo(1)
-        for t in range(PACK):
-            coarse_half(0, t, 1)
+        coarse_half(0, 1)
         order_wc_words(1)
-        order_wc_scales(1)
-        for t in range(PACK - HELD):
-            for h in range(2):
-                coarse_half(1, t, h)
+        order_wc_scales(1, "tab1")
+        load_late()
+        for k in range(1, SLICES):
+            coarse_half(k, 0)
+            coarse_half(k, 1)
+        round_wf_gpsimd(0, 0)
+        round_wf_gpsimd(1, 0)
         gather_tab2(0)
-        load_base(2)
+        pick(0)
+        pick(1)
+        pick(2, "tab20")
         gather_tab2_scales()
+        pick(3)
+        pick(4, "tab2_sc")
         gather_tab2(1)
-        round_wf(0)
-        for t in range(PACK - HELD, PACK):
-            for h in range(2):
-                coarse_half(1, t, h)
-        quantize_wf(0)
-        for t in range(PACK):
-            fine_product(0, t)
-        for b in range(2):
-            for t in range(PACK):
-                pick(b, t)
-        round_wf(1)
-        scaled[0] = staged("scaled0", 9, [P, PACK, M], F32)
-        for t in range(PACK):
-            difference(0, t)
-            scale_picked(0, t)
-        quantize_wf(1)
-        for t in range(PACK):
-            fine_product(1, t)
+        pick(5)
+        pick(6, "tab21")
+        quantize_wf(0, "coarse6")
+        pick(7)
+        for k in range(PACK):
+            scale_pick(k, "wf_bf0")
+        round_wf_scalar(0, 1)
+        round_wf_scalar(1, 1)
         for h in range(2):
-            for t in range(PACK):
-                blend(0, h, t)
-            weave(nc.scalar.copy, 0, h)
-        scaled[1] = staged("scaled1", 9, [P, PACK, M], F32)
-        for t in range(PACK):
-            difference(1, t)
-            scale_picked(1, t)
+            for g in range(2):
+                fine_product(g, h, 4 + 2 * h + g)
+        quantize_wf(1, "wf_w1")
+        for k in range(PACK, SLICES):
+            scale_pick(k, "wf_bf1")
         for h in range(2):
-            quantize_z(0, h)
-            for pair in range(2):
-                height_passes(0, h, pair)
-        for h in range(2):
-            for t in range(PACK):
-                blend(1, h, t)
-        weave(nc.scalar.copy, 1, 0)
-        quantize_z(1, 0)
-        weave(nc.vector.tensor_copy, 1, 1)
-        quantize_z(1, 1)
-        for h in range(2):
-            for pair in range(2):
-                height_passes(1, h, pair)
-                finish(h, pair)
+            for g in range(2):
+                fine_product(2 + g, h, 2 * h + g)
+        difference(0, 0, "wf11")
+        difference(1, 0)
+        difference(0, 1)
+        difference(1, 1)
+        difference(2, 0)
+        difference(3, 0)
+        blend(0, 0, 2)
+        weave(nc.scalar.copy, 0, 0, 2)
+        blend(1, 0, 2)
+        weave(nc.scalar.copy, 1, 0, 2)
+        difference(2, 1)
+        difference(3, 1)
+        blend(0, 2, 2)
+        weave(nc.scalar.copy, 0, 2, 2, "z_bf02")
+        quantize_z(0, 0, 2)
+        quantize_z(1, 0, 2)
+        height_passes(0, 0, 2, (4, 5))
+        height_passes(1, 0, 2, (4, 5))
+        blend(1, 2, 2, "z_rows12")
+        quantize_z(0, 2, 2)
+        height_passes(0, 2, 2, (6, 7))
+        weave(nc.vector.tensor_copy, 1, 2, 2, "z_bf12")
+        finish(0, 2, 0, "z_bf02")
+        quantize_z(1, 2, 2)
+        height_passes(1, 2, 2, (6, 7))
+        finish(0, 2, 1, "z_rows12")
+        finish(2, 2, 0)
+        finish(2, 2, 1)

@@ -140,9 +140,9 @@ def tile_list_lunar_tile_morph_kernel(
         wc_w = [sb("wc_w%d" % b, [P, 2 * PACK * 2 * P], U8) for b in range(2)]
         wc_sc = {}
 
-        def order_wc_scales(b, slot=None):
+        def order_wc_scales(engine, b, slot=None):
             wc_sc[b] = sb("wc_sc%d" % b, [P, 2 * PACK * P], U8, slot)
-            nc.vector.tensor_copy(
+            engine.tensor_copy(
                 wc_sc[b][:].rearrange("p (a t m) -> p a t m", a=2, t=PACK),
                 wc_sc_raw[:].rearrange("p (a b m t) -> p b a t m", a=2, b=2, t=PACK)[:, b],
             )
@@ -181,20 +181,18 @@ def tile_list_lunar_tile_morph_kernel(
         wf_w, wf_sc = {}, {}
         wf_bf = [sb("wf_bf%d" % b, [P, 2 * PACK * PASS], BF16, "wf_bf%d" % b) for b in range(2)]
 
-        def round_wf_scalar(a, b):
-            for u in range(2):
-                nc.scalar.copy(
-                    wf_bf[b][:].rearrange("p (a u e m j) -> p a u m j e", a=2, u=2, e=2, j=PACK)[:, a, u],
-                    wf_raw[a, b][:].rearrange("p j (m u e) -> p u m j e", u=2, e=2)[:, u],
-                )
+        def round_wf_scalar(a, b, u):
+            nc.scalar.copy(
+                wf_bf[b][:].rearrange("p (a u e m j) -> p a u m j e", a=2, u=2, e=2, j=PACK)[:, a, u],
+                wf_raw[a, b][:].rearrange("p j (m u e) -> p u m j e", u=2, e=2)[:, u],
+            )
 
-        def round_wf_gpsimd(a, b):
-            for t in range(0, PACK, 2):
-                nc.gpsimd.tensor_scalar(
-                    wf_bf[b][:].rearrange("p (a t m j) -> p a t m j", a=2, t=PACK, j=PACK)[:, a, t : t + 2],
-                    wf_raw[a, b][:].rearrange("p j (m t) -> p t m j", t=PACK)[:, t : t + 2],
-                    1.0, 0.0, ALU.mult, ALU.add,
-                )
+        def round_wf_gpsimd(a, b, u):
+            nc.gpsimd.tensor_scalar(
+                wf_bf[b][:].rearrange("p (a t m j) -> p a t m j", a=2, t=PACK, j=PACK)[:, a, 2 * u : 2 * u + 2],
+                wf_raw[a, b][:].rearrange("p j (m t) -> p t m j", t=PACK)[:, 2 * u : 2 * u + 2],
+                1.0, 0.0, ALU.mult, ALU.add,
+            )
 
         def quantize_wf(b, slot):
             wf_w[b] = sb("wf_w%d" % b, [P, 2 * PASS], U32, slot)
@@ -210,19 +208,22 @@ def tile_list_lunar_tile_morph_kernel(
         def gather_tab2(a):
             nc.vector.tensor_copy(v2_w[a][:], tab2_w[a][:].indirect(offs2_t[:]))
 
-        picked, scaled, fine, step = {}, {}, {}, {}
+        picked, scaled, fine, diff, step = {}, {}, {}, {}, {}
 
-        def pick(k, slot=None):
-            if k // 2 not in picked:
-                picked[k // 2] = sb("picked%d" % k, [P, 2, M], F32, slot)
+        def carve(name, slot, *parts):
+            whole = sb(name, [P, sum(rows for store, key, rows in parts), M], F32, slot)
+            at = 0
+            for store, key, rows in parts:
+                store[key] = whole[:, at : at + rows, :]
+                at = at + rows
+
+        def pick(k):
             nc.vector.tensor_copy(picked[k // 2][:, k % 2, :], coarse[k][:].indirect(pos_t[:]))
 
-        def scale_pick(k, slot=None):
+        def scale_pick(k):
             b, t = divmod(k, PACK)
-            if b not in scaled:
-                scaled[b] = sb("scaled%d" % b, [P, PACK, M], F32, slot)
             nc.gpsimd.tensor_scalar(
-                scaled[b][:, t, :], picked[k // 2][:, k % 2, :], level_t[:, b, t : t + 1], 0.0, ALU.mult, ALU.add
+                scaled[k][:, 0, :], picked[k // 2][:, k % 2, :], level_t[:, b, t : t + 1], 0.0, ALU.mult, ALU.add
             )
 
         def fine_product(g, h, i):
@@ -242,15 +243,12 @@ def tile_list_lunar_tile_morph_kernel(
                         stop=(a == 1),
                     )
 
-        diffs = {}
-
-        def difference(g, h, slot=None, step_slot=None):
-            if g // 2 not in diffs:
-                diffs[g // 2] = sb("diff%d" % (g // 2), [P, 2, 2, M // 2 * 2], F32, slot)
-            diff = diffs[g // 2][:, h, g % 2, :].rearrange("p (e m) -> p e m", e=2)
-            nc.vector.tensor_tensor(diff[:], fine[g, h][:], picked[g][:, :, HALF * h : HALF * (h + 1)], ALU.subtract)
-            step[g, h] = sb("step%d%d" % (g, h), [P, 2, HALF], F32, step_slot)
-            nc.scalar.activation(step[g, h][:], diff[:], ACT.Tanh)
+        def difference(g, h):
+            nc.vector.tensor_tensor(
+                diff[g, h][:, 0, :].rearrange("p (e m) -> p e m", e=2), fine[g, h][:],
+                picked[g][:, :, HALF * h : HALF * (h + 1)], ALU.subtract,
+            )
+            nc.scalar.activation(step[g, h][:, 0, :], diff[g, h][:, 0, :], ACT.Tanh)
 
         z_rows, z_bf, z_w, z_sc = {}, {}, {}, {}
 
@@ -259,8 +257,8 @@ def tile_list_lunar_tile_morph_kernel(
             h, within = divmod(P * m0, HALF)
             for t in range(PACK):
                 nc.vector.scalar_tensor_tensor(
-                    z_rows[b, m0][:, t, :], step[2 * b + t // 2, h][:, t % 2, within : within + n * P], fade_t[:, b, t : t + 1],
-                    scaled[b][:, t, P * m0 : P * (m0 + n)], ALU.mult, ALU.add,
+                    z_rows[b, m0][:, t, :], step[2 * b + t // 2, h][:, 0, HALF * (t % 2) + within : HALF * (t % 2) + within + n * P],
+                    fade_t[:, b, t : t + 1], scaled[PACK * b + t][:, 0, P * m0 : P * (m0 + n)], ALU.mult, ALU.add,
                 )
 
         def weave(copy, b, m0, n, slot=None):
@@ -277,8 +275,9 @@ def tile_list_lunar_tile_morph_kernel(
 
         height = {}
 
-        def height_passes(b, m0, n, banks):
+        def height_passes(b, source, m0, n, banks):
             per = BANK // (n * P)
+            cols = slice(P * (m0 - source), P * (m0 - source + n))
             for c in range(N // P):
                 if b == 0 and c % per == 0:
                     height[m0, c // per] = bank(banks[c // per], "height", [P, per, n * P])
@@ -286,8 +285,8 @@ def tile_list_lunar_tile_morph_kernel(
                     out=height[m0, c // per][:, c % per, :],
                     lhsT=late["wo"][:, N * b + P * c : N * b + P * (c + 1)].bitcast(FP8X4),
                     lhsT_scale=wo_sc[4 * b : P, P * c : P * (c + 1)],
-                    rhs=z_w[b, m0][:].bitcast(FP8X4),
-                    rhs_scale=z_sc[b, m0][:],
+                    rhs=z_w[b, source][:, cols].bitcast(FP8X4),
+                    rhs_scale=z_sc[b, source][:, cols],
                     start=(b == 0 and c % per == 0),
                     stop=(b == 1 and c % per == per - 1),
                 )
@@ -304,69 +303,77 @@ def tile_list_lunar_tile_morph_kernel(
         order_wc_words(0)
         gather_tab(0, 0)
         gather_tab(0, 1)
-        order_wc_scales(0)
+        order_wc_scales(nc.gpsimd, 0)
+        order_wc_scales(nc.gpsimd, 1)
         gather_tab(1, 0)
         coarse_half(0, 0)
         gather_tab(1, 1)
         coarse_half(0, 1)
         order_wc_words(1)
-        order_wc_scales(1, "tab1")
         load_late()
         for k in range(1, SLICES):
             coarse_half(k, 0)
             coarse_half(k, 1)
-        round_wf_gpsimd(0, 0)
-        round_wf_gpsimd(1, 0)
+        round_wf_gpsimd(0, 0, 0)
+        round_wf_gpsimd(0, 0, 1)
+        round_wf_gpsimd(1, 0, 0)
+        round_wf_scalar(1, 0, 1)
         gather_tab2(0)
+        carve("picked0", "tab20", (picked, 0, 2))
         pick(0)
         pick(1)
-        pick(2, "tab20")
         gather_tab2_scales()
-        pick(3)
-        pick(4, "tab2_sc")
+        carve("picked1", "tab2_sc", (picked, 1, 2), (picked, 2, 2))
+        for k in range(2, 6):
+            pick(k)
+        carve("scaled0", "wf00", (scaled, 0, 1), (scaled, 1, 1), (scaled, 2, 1))
+        for k in range(3):
+            scale_pick(k)
         gather_tab2(1)
-        pick(5)
-        pick(6, "tab21")
-        quantize_wf(0, "coarse6")
+        quantize_wf(0, "tab21")
+        carve("after_wf0", "wf_bf0", (picked, 3, 2), (scaled, 3, 1), (scaled, 4, 1), (scaled, 5, 1))
+        pick(6)
         pick(7)
-        for k in range(PACK):
-            scale_pick(k, "wf_bf0")
-        round_wf_scalar(0, 1)
-        round_wf_scalar(1, 1)
+        for k in range(3, 6):
+            scale_pick(k)
+        for a in range(2):
+            for u in range(2):
+                round_wf_scalar(a, 1, u)
         for h in range(2):
             for g in range(2):
                 fine_product(g, h, 4 + 2 * h + g)
         quantize_wf(1, "wf_w1")
-        for k in range(PACK, SLICES):
-            scale_pick(k, "wf_bf1")
+        carve("after_wf1", "wf_bf1", (scaled, 6, 1), (scaled, 7, 1))
+        scale_pick(6)
+        scale_pick(7)
         for h in range(2):
             for g in range(2):
                 fine_product(2 + g, h, 2 * h + g)
-        difference(0, 0, "wf11")
-        difference(1, 0)
-        difference(0, 1)
-        difference(1, 1)
-        difference(2, 0)
-        difference(3, 0)
+        carve("diffs0", "wf11", (diff, (0, 0), 1), (diff, (1, 0), 1), (diff, (0, 1), 1), (diff, (1, 1), 1))
+        carve("steps0", "steps0", (step, (0, 0), 1), (step, (1, 0), 1), (step, (0, 1), 1), (step, (1, 1), 1))
+        carve("diffs1", "wf01", (diff, (2, 0), 1), (diff, (3, 0), 1), (diff, (2, 1), 1), (diff, (3, 1), 1))
+        carve("steps1", "wf10", (step, (2, 0), 1), (step, (3, 0), 1), (step, (2, 1), 1), (step, (3, 1), 1))
+        for g, h in ((0, 0), (1, 0), (0, 1), (1, 1), (2, 0), (3, 0)):
+            difference(g, h)
         blend(0, 0, 2)
         weave(nc.scalar.copy, 0, 0, 2)
         blend(1, 0, 2)
-        weave(nc.scalar.copy, 1, 0, 2)
         difference(2, 1)
         difference(3, 1)
+        weave(nc.scalar.copy, 1, 0, 2)
         blend(0, 2, 2)
         weave(nc.scalar.copy, 0, 2, 2, "z_bf02")
         quantize_z(0, 0, 2)
         quantize_z(1, 0, 2)
-        height_passes(0, 0, 2, (4, 5))
-        height_passes(1, 0, 2, (4, 5))
+        height_passes(0, 0, 0, 2, (4, 5))
+        height_passes(1, 0, 0, 2, (4, 5))
         blend(1, 2, 2, "z_rows12")
         quantize_z(0, 2, 2)
-        height_passes(0, 2, 2, (6, 7))
+        height_passes(0, 2, 2, 2, (6, 7))
         weave(nc.vector.tensor_copy, 1, 2, 2, "z_bf12")
         finish(0, 2, 0, "z_bf02")
         quantize_z(1, 2, 2)
-        height_passes(1, 2, 2, (6, 7))
+        height_passes(1, 2, 2, 2, (6, 7))
         finish(0, 2, 1, "z_rows12")
         finish(2, 2, 0)
         finish(2, 2, 1)

@@ -81,7 +81,7 @@ def tile_list_lunar_tile_morph_kernel(
             )
 
         def load_wc_scales(queue):
-            for q in range(QUADS):
+            for q in (0, 2, 1, 3):
                 queue.dma_start(
                     out=wc_sc_raw[32 * q : 32 * q + 4, :].bitcast(I32).rearrange("r (a c) -> r a c", a=2),
                     in_=wc_scales[:, 4 * q : 4 * q + 4, :].bitcast(I32).rearrange("a r c -> r a c"),
@@ -121,9 +121,9 @@ def tile_list_lunar_tile_morph_kernel(
         load_planes_packed(nc.sync, tab2_sc, tab2_scales)
         load_wf(1, 0)
         load_factors()
-        load_words(tab2_w[1], tab2_words[1])
         load_wf(0, 1)
         load_wf(1, 1)
+        load_words(tab2_w[1], tab2_words[1])
 
         late = {}
 
@@ -189,15 +189,17 @@ def tile_list_lunar_tile_morph_kernel(
 
         def round_wf_gpsimd(a, b, u):
             nc.gpsimd.tensor_scalar(
-                wf_bf[b][:].rearrange("p (a t m j) -> p a t m j", a=2, t=PACK, j=PACK)[:, a, 2 * u : 2 * u + 2],
-                wf_raw[a, b][:].rearrange("p j (m t) -> p t m j", t=PACK)[:, 2 * u : 2 * u + 2],
+                wf_bf[b][:].rearrange("p (a u e m j) -> p a u m e j", a=2, u=2, e=2, j=PACK)[:, a, u],
+                wf_raw[a, b][:].rearrange("p j (m u e) -> p u m e j", u=2, e=2)[:, u],
                 1.0, 0.0, ALU.mult, ALU.add,
             )
 
         def quantize_wf(b, slot):
-            wf_w[b] = sb("wf_w%d" % b, [P, 2 * PASS], U32, slot)
+            wf_w[b] = sb("wf_w%d" % b, [P, 2, PASS], U32, slot)
             wf_sc[b] = sb("wf_sc%d" % b, [P, 2 * PASS], U8)
-            nc.vector.quantize_mx(out=wf_w[b][:].bitcast(FP8X4), scales=wf_sc[b][:], in_=wf_bf[b][:])
+            nc.vector.quantize_mx(
+                out=wf_w[b][:].rearrange("p a c -> p (a c)").bitcast(FP8X4), scales=wf_sc[b][:], in_=wf_bf[b][:]
+            )
 
         v2_sc = sb("v2_sc", [P, M], U8)
         v2_w = [sb("v2_w%d" % a, [P, M], U32) for a in range(2)]
@@ -226,22 +228,25 @@ def tile_list_lunar_tile_morph_kernel(
                 scaled[k][:, 0, :], picked[k // 2][:, k % 2, :], level_t[:, b, t : t + 1], 0.0, ALU.mult, ALU.add
             )
 
-        def fine_product(g, h, i):
-            fine[g, h] = bank(i, "fine", [P, 2, HALF])
+        def scale_pick_scalar(k):
+            b, t = divmod(k, PACK)
+            nc.scalar.activation(scaled[k][:, 0, :], picked[k // 2][:, k % 2, :], ACT.Copy, scale=level_t[:, b, t : t + 1])
+
+        def fine_passes(g, h, a, i=None):
+            if a == 0:
+                fine[g, h] = bank(i, "fine", [P, 2, HALF])
             cols_m = slice(HALF * h, HALF * (h + 1))
             for e in range(2):
                 b, t = divmod(2 * g + e, PACK)
-                for a in range(2):
-                    cols = slice(PASS * a + P * t, PASS * a + P * (t + 1))
-                    nc.tensor.matmul_mx(
-                        out=fine[g, h][:, e, :],
-                        lhsT=wf_w[b][:, cols].bitcast(FP8X4),
-                        lhsT_scale=wf_sc[b][:, cols],
-                        rhs=v2_w[a][:, cols_m].bitcast(FP8X4),
-                        rhs_scale=v2_sc[4 * a : P, cols_m],
-                        start=(a == 0),
-                        stop=(a == 1),
-                    )
+                nc.tensor.matmul_mx(
+                    out=fine[g, h][:, e, :],
+                    lhsT=wf_w[b][:, a, P * t : P * (t + 1)].bitcast(FP8X4),
+                    lhsT_scale=wf_sc[b][:, PASS * a + P * t : PASS * a + P * (t + 1)],
+                    rhs=v2_w[a][:, cols_m].bitcast(FP8X4),
+                    rhs_scale=v2_sc[4 * a : P, cols_m],
+                    start=(a == 0 and e == 0),
+                    stop=(a == 1 and e == 1),
+                )
 
         def difference(g, h):
             nc.vector.tensor_tensor(
@@ -291,14 +296,17 @@ def tile_list_lunar_tile_morph_kernel(
                     stop=(b == 1 and c % per == per - 1),
                 )
 
-        def finish(m0, n, i, slot=None):
+        results = {}
+
+        def finish(m0, n, i, first, count):
             per = BANK // (n * P)
             cols = slice(P * m0, P * (m0 + n))
-            result = sb("result%d%d" % (m0, i), [P, per, n * P], F32, slot)
-            nc.vector.tensor_tensor(result[:], height[m0, i][:], late["base"][:, per * i : per * (i + 1), cols], ALU.add)
-            nc.sync.dma_start(
-                out=out[per * P * i : per * P * (i + 1), cols].rearrange("(i p) m -> p i m", p=P), in_=result[:]
+            c0 = per * i + first
+            result = results[m0, i][:, 0, :].rearrange("p (c m) -> p c m", c=per)[:, first : first + count, :]
+            nc.vector.tensor_tensor(
+                result, height[m0, i][:, first : first + count, :], late["base"][:, c0 : c0 + count, cols], ALU.add
             )
+            nc.sync.dma_start(out=out[P * c0 : P * (c0 + count), cols].rearrange("(i p) m -> p i m", p=P), in_=result)
 
         order_wc_words(0)
         gather_tab(0, 0)
@@ -323,57 +331,58 @@ def tile_list_lunar_tile_morph_kernel(
         pick(0)
         pick(1)
         gather_tab2_scales()
-        carve("picked1", "tab2_sc", (picked, 1, 2), (picked, 2, 2))
+        carve("picked1", "picked1", (picked, 1, 2), (picked, 2, 2))
         for k in range(2, 6):
             pick(k)
-        carve("scaled0", "wf00", (scaled, 0, 1), (scaled, 1, 1), (scaled, 2, 1))
-        for k in range(3):
-            scale_pick(k)
-        gather_tab2(1)
-        quantize_wf(0, "tab21")
-        carve("after_wf0", "wf_bf0", (picked, 3, 2), (scaled, 3, 1), (scaled, 4, 1), (scaled, 5, 1))
+        quantize_wf(0, "coarse4")
+        carve("after_wf0", "wf_bf0", (picked, 3, 2), *[(scaled, k, 1) for k in range(PACK)])
         pick(6)
         pick(7)
-        for k in range(3, 6):
+        for k in range(PACK):
             scale_pick(k)
         for a in range(2):
             for u in range(2):
                 round_wf_scalar(a, 1, u)
+        gather_tab2(1)
+        for a in range(2):
+            for h in range(2):
+                for g in range(2):
+                    fine_passes(g, h, a, 4 + 2 * h + g)
+        quantize_wf(1, "tab21")
+        carve("after_wf1", "wf_bf1", *[(scaled, k, 1) for k in range(PACK, SLICES)])
+        for k in range(PACK, SLICES):
+            scale_pick(k)
         for h in range(2):
             for g in range(2):
-                fine_product(g, h, 4 + 2 * h + g)
-        quantize_wf(1, "wf_w1")
-        carve("after_wf1", "wf_bf1", (scaled, 6, 1), (scaled, 7, 1))
-        scale_pick(6)
-        scale_pick(7)
-        for h in range(2):
-            for g in range(2):
-                fine_product(2 + g, h, 2 * h + g)
+                for a in range(2):
+                    fine_passes(2 + g, h, a, 2 * h + g)
         carve("diffs0", "wf11", (diff, (0, 0), 1), (diff, (1, 0), 1), (diff, (0, 1), 1), (diff, (1, 1), 1))
-        carve("steps0", "steps0", (step, (0, 0), 1), (step, (1, 0), 1), (step, (0, 1), 1), (step, (1, 1), 1))
+        carve("steps0", "wf00", (step, (0, 0), 1), (step, (1, 0), 1), (step, (0, 1), 1), (step, (1, 1), 1))
         carve("diffs1", "wf01", (diff, (2, 0), 1), (diff, (3, 0), 1), (diff, (2, 1), 1), (diff, (3, 1), 1))
         carve("steps1", "wf10", (step, (2, 0), 1), (step, (3, 0), 1), (step, (2, 1), 1), (step, (3, 1), 1))
         for g, h in ((0, 0), (1, 0), (0, 1), (1, 1), (2, 0), (3, 0)):
             difference(g, h)
         blend(0, 0, 2)
-        weave(nc.scalar.copy, 0, 0, 2)
+        weave(nc.scalar.copy, 0, 0, 2, "z_bf00")
         blend(1, 0, 2)
+        weave(nc.scalar.copy, 1, 0, 2)
         difference(2, 1)
         difference(3, 1)
-        weave(nc.scalar.copy, 1, 0, 2)
         blend(0, 2, 2)
-        weave(nc.scalar.copy, 0, 2, 2, "z_bf02")
+        weave(nc.scalar.copy, 0, 2, 2)
         quantize_z(0, 0, 2)
         quantize_z(1, 0, 2)
         height_passes(0, 0, 0, 2, (4, 5))
         height_passes(1, 0, 0, 2, (4, 5))
-        blend(1, 2, 2, "z_rows12")
+        blend(1, 2, 2, "z_bf00")
         quantize_z(0, 2, 2)
         height_passes(0, 2, 2, 2, (6, 7))
-        weave(nc.vector.tensor_copy, 1, 2, 2, "z_bf12")
-        finish(0, 2, 0, "z_bf02")
+        weave(nc.vector.tensor_copy, 1, 2, 2)
         quantize_z(1, 2, 2)
         height_passes(1, 2, 2, 2, (6, 7))
-        finish(0, 2, 1, "z_rows12")
-        finish(2, 2, 0)
-        finish(2, 2, 1)
+        carve("results0", "z_bf00", (results, (0, 0), 1), (results, (0, 1), 1))
+        carve("results1", "results1", (results, (2, 0), 1), (results, (2, 1), 1))
+        finish(0, 2, 0, 0, 2)
+        finish(0, 2, 1, 0, 2)
+        finish(2, 2, 0, 0, 2)
+        finish(2, 2, 1, 0, 2)

@@ -219,18 +219,23 @@ def tile_list_lunar_tile_morph_kernel(
                 store[key] = whole[:, at : at + rows, :]
                 at = at + rows
 
+        alone = {}
+
+        def one_pick(k):
+            return alone[k][:, 0, :] if k in alone else picked[k // 2][:, k % 2, :]
+
         def pick(k):
-            nc.vector.tensor_copy(picked[k // 2][:, k % 2, :], coarse[k][:].indirect(pos_t[:]))
+            nc.vector.tensor_copy(one_pick(k), coarse[k][:].indirect(pos_t[:]))
 
         def scale_pick(k):
             b, t = divmod(k, PACK)
             nc.gpsimd.tensor_scalar(
-                scaled[k][:, 0, :], picked[k // 2][:, k % 2, :], level_t[:, b, t : t + 1], 0.0, ALU.mult, ALU.add
+                scaled[k][:, 0, :], one_pick(k), level_t[:, b, t : t + 1], 0.0, ALU.mult, ALU.add
             )
 
         def scale_pick_scalar(k):
             b, t = divmod(k, PACK)
-            nc.scalar.activation(scaled[k][:, 0, :], picked[k // 2][:, k % 2, :], ACT.Copy, scale=level_t[:, b, t : t + 1])
+            nc.scalar.activation(scaled[k][:, 0, :], one_pick(k), ACT.Copy, scale=level_t[:, b, t : t + 1])
 
         def fine_passes(g, h, a, i=None):
             if a == 0:
@@ -249,10 +254,13 @@ def tile_list_lunar_tile_morph_kernel(
                 )
 
         def difference(g, h):
-            nc.vector.tensor_tensor(
-                diff[g, h][:, 0, :].rearrange("p (e m) -> p e m", e=2), fine[g, h][:],
-                picked[g][:, :, HALF * h : HALF * (h + 1)], ALU.subtract,
-            )
+            cols = slice(HALF * h, HALF * (h + 1))
+            both = diff[g, h][:, 0, :].rearrange("p (e m) -> p e m", e=2)
+            if g in picked:
+                nc.vector.tensor_tensor(both, fine[g, h][:], picked[g][:, :, cols], ALU.subtract)
+            else:
+                for e in range(2):
+                    nc.vector.tensor_tensor(both[:, e, :], fine[g, h][:, e, :], one_pick(2 * g + e)[:, cols], ALU.subtract)
             nc.scalar.activation(step[g, h][:, 0, :], diff[g, h][:, 0, :], ACT.Tanh)
 
         z_rows, z_bf, z_w, z_sc = {}, {}, {}, {}
@@ -334,15 +342,18 @@ def tile_list_lunar_tile_morph_kernel(
         carve("picked1", "picked1", (picked, 1, 2), (picked, 2, 2))
         for k in range(2, 6):
             pick(k)
-        quantize_wf(0, "coarse4")
-        carve("after_wf0", "wf_bf0", (picked, 3, 2), *[(scaled, k, 1) for k in range(PACK)])
+        carve("pick6", "pick6", (alone, 6, 1))
         pick(6)
+        quantize_wf(0, "coarse5")
+        carve("after_wf0", "wf_bf0", (alone, 7, 1), *[(scaled, k, 1) for k in range(3)])
         pick(7)
-        for k in range(PACK):
+        for k in range(3):
             scale_pick(k)
         for a in range(2):
             for u in range(2):
                 round_wf_scalar(a, 1, u)
+        carve("after_round", "wf11", (scaled, 3, 1))
+        scale_pick_scalar(3)
         gather_tab2(1)
         for a in range(2):
             for h in range(2):
@@ -356,7 +367,7 @@ def tile_list_lunar_tile_morph_kernel(
             for g in range(2):
                 for a in range(2):
                     fine_passes(2 + g, h, a, 2 * h + g)
-        carve("diffs0", "wf11", (diff, (0, 0), 1), (diff, (1, 0), 1), (diff, (0, 1), 1), (diff, (1, 1), 1))
+        carve("diffs0", "diffs0", (diff, (0, 0), 1), (diff, (1, 0), 1), (diff, (0, 1), 1), (diff, (1, 1), 1))
         carve("steps0", "wf00", (step, (0, 0), 1), (step, (1, 0), 1), (step, (0, 1), 1), (step, (1, 1), 1))
         carve("diffs1", "wf01", (diff, (2, 0), 1), (diff, (3, 0), 1), (diff, (2, 1), 1), (diff, (3, 1), 1))
         carve("steps1", "wf10", (step, (2, 0), 1), (step, (3, 0), 1), (step, (2, 1), 1), (step, (3, 1), 1))

@@ -24,6 +24,7 @@ HALF = M // 2
 QUADS = 4
 SLICES = H // P
 LIVE = 32 * (QUADS - 1) + 4
+APART = 16
 
 
 def tile_list_lunar_tile_morph_kernel(
@@ -53,6 +54,16 @@ def tile_list_lunar_tile_morph_kernel(
                     in_=scales[:, 4 * q : 4 * q + 4, :].bitcast(I32),
                 )
 
+        def load_planes_spread(tile, scales):
+            for r in range(4):
+                nc.sync.dma_start(
+                    out=tile[r:P:APART, :].bitcast(I32),
+                    in_=scales[:, r:16:4, :].bitcast(I32).rearrange("a q n -> q a n"),
+                )
+
+        def lower_second_plane(plane, both):
+            nc.sync.dma_start(out=plane[0:LIVE, :].bitcast(I32), in_=both[APART : APART + LIVE, :].bitcast(I32))
+
         def load_words(tile, words):
             nc.sync.dma_start(out=tile[:].bitcast(I32), in_=words.rearrange("p t i -> p (t i)").bitcast(I32))
 
@@ -64,14 +75,15 @@ def tile_list_lunar_tile_morph_kernel(
         wc_sc_raw = sb("wc_sc_raw", [P, 2 * H], U8, "wc_sc_raw")
         tab2_sc = sb("tab2_sc", [P, T], U8, "tab2_sc")
         v_sc = [sb("v_sc%d" % a, [P, S], U8) for a in range(2)]
+        v2_sc = [sb("v2_sc%d" % a, [P, M], U8) for a in range(2)]
         wo_sc = sb("wo_sc", [P, N], U8)
         zero(nc.gpsimd, tab_sc)
-        for tile in (wc_sc_raw, tab2_sc, v_sc[1], wo_sc):
+        for tile in (wc_sc_raw, tab2_sc, v_sc[1], v2_sc[1], wo_sc):
             zero(nc.vector, tile)
 
         nc.sync.dma_start(offs_t[:], offs)
         nc.sync.dma_start(pos_t[:], pos1)
-        load_planes_packed(nc.sync, tab_sc, tab_scales)
+        load_planes_spread(tab_sc, tab_scales)
         wc_raw = [sb("wc_raw%d" % b, [P, 2 * 2 * PASS], U8, "wc_raw%d" % b) for b in range(2)]
 
         def load_wc(b):
@@ -81,10 +93,10 @@ def tile_list_lunar_tile_morph_kernel(
             )
 
         def load_wc_scales(queue):
-            for q in (0, 2, 1, 3):
+            for r in range(4):
                 queue.dma_start(
-                    out=wc_sc_raw[32 * q : 32 * q + 4, :].bitcast(I32).rearrange("r (a c) -> r a c", a=2),
-                    in_=wc_scales[:, 4 * q : 4 * q + 4, :].bitcast(I32).rearrange("a r c -> r a c"),
+                    out=wc_sc_raw[r:P:32, :].bitcast(I32).rearrange("q (a c) -> q a c", a=2),
+                    in_=wc_scales[:, r:16:4, :].bitcast(I32).rearrange("a q c -> q a c"),
                 )
 
         wf_raw = {}
@@ -101,29 +113,34 @@ def tile_list_lunar_tile_morph_kernel(
         level_t = sb("level_t", [P, 2, PACK], F32)
         fade_t = sb("fade_t", [P, 2, PACK], F32)
 
-        def load_factors():
-            nc.sync.dma_start(out=level_t[:], in_=level.rearrange("(b p t) -> p b t", b=2, t=PACK))
-            nc.sync.dma_start(out=fade_t[:], in_=fade.rearrange("(b p t) -> p b t", b=2, t=PACK))
+        def load_factor(tile, values):
+            nc.sync.dma_start(out=tile[:], in_=values.rearrange("(b p t) -> p b t", b=2, t=PACK))
+
+        def gather_tab2_scales():
+            nc.vector.tensor_copy(v2_sc[0][:], tab2_sc[:].indirect(offs2_t[:]))
+            lower_second_plane(v2_sc[1], v2_sc[0])
 
         def gather_tab_scales():
             nc.vector.tensor_copy(v_sc[0][:], tab_sc[:].indirect(offs_t[:]))
-            nc.sync.dma_start(out=v_sc[1][0:LIVE, :].bitcast(I32), in_=v_sc[0][4 : 4 + LIVE, :].bitcast(I32))
+            lower_second_plane(v_sc[1], v_sc[0])
 
         load_wc(0)
         load_words(tab_w[0], tab_words[0])
         load_wc_scales(nc.sync)
         load_words(tab_w[1], tab_words[1])
         gather_tab_scales()
-        load_wc(1)
-        load_words(tab2_w[0], tab2_words[0])
         nc.sync.dma_start(offs2_t[:], offs2)
+        load_wc(1)
+        load_planes_spread(tab2_sc, tab2_scales)
         load_wf(0, 0)
-        load_planes_packed(nc.sync, tab2_sc, tab2_scales)
         load_wf(1, 0)
-        load_factors()
+        load_words(tab2_w[0], tab2_words[0])
+        gather_tab2_scales()
+        load_factor(level_t, level)
         load_wf(0, 1)
         load_wf(1, 1)
         load_words(tab2_w[1], tab2_words[1])
+        load_factor(fade_t, fade)
 
         late = {}
 
@@ -201,11 +218,7 @@ def tile_list_lunar_tile_morph_kernel(
                 out=wf_w[b][:].rearrange("p a c -> p (a c)").bitcast(FP8X4), scales=wf_sc[b][:], in_=wf_bf[b][:]
             )
 
-        v2_sc = sb("v2_sc", [P, M], U8)
         v2_w = [sb("v2_w%d" % a, [P, M], U32) for a in range(2)]
-
-        def gather_tab2_scales():
-            nc.vector.tensor_copy(v2_sc[:], tab2_sc[:].indirect(offs2_t[:]))
 
         def gather_tab2(a):
             nc.vector.tensor_copy(v2_w[a][:], tab2_w[a][:].indirect(offs2_t[:]))
@@ -248,7 +261,7 @@ def tile_list_lunar_tile_morph_kernel(
                     lhsT=wf_w[b][:, a, P * t : P * (t + 1)].bitcast(FP8X4),
                     lhsT_scale=wf_sc[b][:, PASS * a + P * t : PASS * a + P * (t + 1)],
                     rhs=v2_w[a][:, cols_m].bitcast(FP8X4),
-                    rhs_scale=v2_sc[4 * a : P, cols_m],
+                    rhs_scale=v2_sc[a][:, cols_m],
                     start=(a == 0 and e == 0),
                     stop=(a == 1 and e == 1),
                 )
@@ -333,15 +346,15 @@ def tile_list_lunar_tile_morph_kernel(
         round_wf_gpsimd(0, 0, 0)
         round_wf_gpsimd(0, 0, 1)
         round_wf_gpsimd(1, 0, 0)
-        round_wf_scalar(1, 0, 1)
-        gather_tab2(0)
-        carve("picked0", "tab20", (picked, 0, 2))
+        round_wf_gpsimd(1, 0, 1)
+        carve("picked0", "tab2_sc", (picked, 0, 2), (picked, 1, 2))
         pick(0)
         pick(1)
-        gather_tab2_scales()
-        carve("picked1", "picked1", (picked, 1, 2), (picked, 2, 2))
-        for k in range(2, 6):
+        carve("picked1", "picked1", (picked, 2, 2))
+        for k in range(2, 5):
             pick(k)
+        gather_tab2(0)
+        pick(5)
         carve("pick6", "pick6", (alone, 6, 1))
         pick(6)
         quantize_wf(0, "coarse5")

@@ -170,6 +170,12 @@ def tile_list_lunar_tile_morph_kernel(
                 wc_raw[b][:].bitcast(U16).rearrange("p (a m t) -> p a t m", a=2, t=PACK),
             )
 
+        def order_wc_words_gpsimd(b):
+            nc.gpsimd.tensor_copy(
+                wc_w[b][:].rearrange("p (a t m e) -> p a t m e", a=2, t=PACK, e=2),
+                wc_raw[b][:].rearrange("p (a m t e) -> p a t m e", a=2, t=PACK, e=2),
+            )
+
         v_w = {}
 
         def gather_tab(a, h, slot=None):
@@ -329,16 +335,16 @@ def tile_list_lunar_tile_morph_kernel(
             )
             nc.sync.dma_start(out=out[P * c0 : P * (c0 + count), cols].rearrange("(i p) m -> p i m", p=P), in_=result)
 
-        order_wc_words(0)
-        gather_tab(0, 0)
-        gather_tab(0, 1)
+        order_wc_words_gpsimd(0)
         order_wc_scales(nc.gpsimd, 0)
         order_wc_scales(nc.gpsimd, 1)
+        order_wc_words_gpsimd(1)
+        gather_tab(0, 0)
+        gather_tab(0, 1)
         gather_tab(1, 0)
         coarse_half(0, 0)
         gather_tab(1, 1)
         coarse_half(0, 1)
-        order_wc_words(1)
         load_late()
         for k in range(1, SLICES):
             coarse_half(k, 0)
@@ -346,7 +352,7 @@ def tile_list_lunar_tile_morph_kernel(
         round_wf_gpsimd(0, 0, 0)
         round_wf_gpsimd(0, 0, 1)
         round_wf_gpsimd(1, 0, 0)
-        round_wf_gpsimd(1, 0, 1)
+        round_wf_scalar(1, 0, 1)
         carve("picked0", "tab2_sc", (picked, 0, 2), (picked, 1, 2))
         pick(0)
         pick(1)
@@ -398,15 +404,21 @@ def tile_list_lunar_tile_morph_kernel(
         quantize_z(1, 0, 2)
         height_passes(0, 0, 0, 2, (4, 5))
         height_passes(1, 0, 0, 2, (4, 5))
-        blend(1, 2, 2, "z_bf00")
+        blend(1, 2, 1, "z_bf00")
+        weave(nc.scalar.copy, 1, 2, 1)
+        blend(1, 3, 1, "z_rows13")
         quantize_z(0, 2, 2)
-        height_passes(0, 2, 2, 2, (6, 7))
-        weave(nc.vector.tensor_copy, 1, 2, 2)
-        quantize_z(1, 2, 2)
-        height_passes(1, 2, 2, 2, (6, 7))
-        carve("results0", "z_bf00", (results, (0, 0), 1), (results, (0, 1), 1))
-        carve("results1", "results1", (results, (2, 0), 1), (results, (2, 1), 1))
+        height_passes(0, 2, 2, 1, (6,))
+        height_passes(0, 2, 3, 1, (7,))
+        weave(nc.vector.tensor_copy, 1, 3, 1)
+        quantize_z(1, 2, 1)
+        height_passes(1, 2, 2, 1, (6,))
+        quantize_z(1, 3, 1)
+        height_passes(1, 3, 3, 1, (7,))
+        carve("results0", "z_rows13", (results, (0, 0), 1), (results, (0, 1), 1))
+        carve("results1", "results1", (results, (2, 0), 1), (results, (3, 0), 1))
         finish(0, 2, 0, 0, 2)
         finish(0, 2, 1, 0, 2)
-        finish(2, 2, 0, 0, 2)
-        finish(2, 2, 1, 0, 2)
+        finish(2, 1, 0, 0, 4)
+        finish(3, 1, 0, 0, 2)
+        finish(3, 1, 0, 2, 2)

@@ -157,12 +157,14 @@ def tile_list_lunar_tile_morph_kernel(
         wc_w = [sb("wc_w%d" % b, [P, 2 * PACK * 2 * P], U8) for b in range(2)]
         wc_sc = {}
 
-        def order_wc_scales(engine, b, slot=None):
-            wc_sc[b] = sb("wc_sc%d" % b, [P, 2 * PACK * P], U8, slot)
-            engine.tensor_copy(
-                wc_sc[b][:].rearrange("p (a t m) -> p a t m", a=2, t=PACK),
-                wc_sc_raw[:].rearrange("p (a b m t) -> p b a t m", a=2, b=2, t=PACK)[:, b],
-            )
+        def order_wc_scales(b, pieces):
+            wc_sc[b] = sb("wc_sc%d" % b, [P, 2 * PACK * P], U8)
+            for t0 in range(0, PACK, PACK // pieces):
+                ts = slice(t0, t0 + PACK // pieces)
+                nc.gpsimd.tensor_copy(
+                    wc_sc[b][:].rearrange("p (t a m) -> p t a m", a=2, t=PACK)[:, ts],
+                    wc_sc_raw[:].rearrange("p (a b m t) -> p b t a m", a=2, b=2, t=PACK)[:, b, ts],
+                )
 
         def order_wc_words(b):
             nc.vector.tensor_copy(
@@ -170,17 +172,25 @@ def tile_list_lunar_tile_morph_kernel(
                 wc_raw[b][:].bitcast(U16).rearrange("p (a m t) -> p a t m", a=2, t=PACK),
             )
 
-        def order_wc_words_gpsimd(b):
-            nc.gpsimd.tensor_copy(
-                wc_w[b][:].rearrange("p (a t m e) -> p a t m e", a=2, t=PACK, e=2),
-                wc_raw[b][:].rearrange("p (a m t e) -> p a t m e", a=2, t=PACK, e=2),
-            )
+        def order_wc_words_gpsimd(b, pieces):
+            for t0 in range(0, PACK, PACK // pieces):
+                ts = slice(t0, t0 + PACK // pieces)
+                nc.gpsimd.tensor_copy(
+                    wc_w[b][:].rearrange("p (t a m e) -> p t a m e", a=2, t=PACK, e=2)[:, ts],
+                    wc_raw[b][:].rearrange("p (a m t e) -> p t a m e", a=2, t=PACK, e=2)[:, ts],
+                )
 
         v_w = {}
 
         def gather_tab(a, h, slot=None):
             v_w[a, h] = sb("v_w%d%d" % (a, h), [P, BANK], U32, slot)
             nc.vector.tensor_copy(v_w[a, h][:], tab_w[a][:].indirect(offs_t[:, 32 * h : 32 * (h + 1)]))
+
+        def gather_tab_whole(a):
+            whole = sb("v_w%d" % a, [P, S], U32)
+            nc.vector.tensor_copy(whole[:], tab_w[a][:].indirect(offs_t[:]))
+            for h in range(2):
+                v_w[a, h] = whole[:, BANK * h : BANK * (h + 1)]
 
         coarse = [sb("coarse%d" % k, [P, S], F32, "coarse%d" % k) for k in range(SLICES)]
 
@@ -189,7 +199,7 @@ def tile_list_lunar_tile_morph_kernel(
             acc = bank((2 * k + h) % 4, "acc", [P, BANK])
             cols = slice(BANK * h, BANK * (h + 1))
             for a in range(2):
-                place = a * PACK + t
+                place = 2 * t + a
                 nc.tensor.matmul_mx(
                     out=acc[:],
                     lhsT=wc_w[b][:, 2 * P * place : 2 * P * (place + 1)].bitcast(FP4X4),
@@ -335,12 +345,11 @@ def tile_list_lunar_tile_morph_kernel(
             )
             nc.sync.dma_start(out=out[P * c0 : P * (c0 + count), cols].rearrange("(i p) m -> p i m", p=P), in_=result)
 
-        order_wc_words_gpsimd(0)
-        order_wc_scales(nc.gpsimd, 0)
-        order_wc_scales(nc.gpsimd, 1)
-        order_wc_words_gpsimd(1)
-        gather_tab(0, 0)
-        gather_tab(0, 1)
+        order_wc_words_gpsimd(0, 1)
+        order_wc_scales(0, 2)
+        order_wc_scales(1, 1)
+        order_wc_words_gpsimd(1, 2)
+        gather_tab_whole(0)
         gather_tab(1, 0)
         coarse_half(0, 0)
         gather_tab(1, 1)

from contextlib import ExitStack

import concourse.mybir as mybir

K, H, N, T, S, M = 1024, 1024, 512, 2048, 1024, 512
FLOPS = 2 * K * H * S + 2 * K * H * M + 2 * H * N * M

F32 = mybir.dt.float32
BF16 = mybir.dt.bfloat16
I32 = mybir.dt.int32
U32 = mybir.dt.uint32
U16 = mybir.dt.uint16
U8 = mybir.dt.uint8
FP8X4 = mybir.dt.float8_e4m3fn_x4
FP4X4 = mybir.dt.float4_e2m1fn_x4
ACT = mybir.ActivationFunctionType
ALU = mybir.AluOpType

P = 128
PACK = 4
PASS = P * PACK
BANK = 512
HALF = M // 2
QUADS = 4
SLICES = H // P
LIVE = 32 * (QUADS - 1) + 4
APART = 16


def tile_list_lunar_tile_morph_kernel(
    tc, tab_words, tab_scales, offs, pos1, tab2_words, tab2_scales, offs2,
    wc_words, wc_scales, wf, wo_words, wo_scales, level, fade, base, out,
):
    nc = tc.nc
    with ExitStack() as ctx:
        keep = ctx.enter_context(tc.tile_pool(name="keep", bufs=1))
        psum = ctx.enter_context(tc.psum_pool(name="psum", bufs=1))

        def sb(name, shape, dtype, slot=None):
            if slot is None:
                return keep.tile(shape, dtype, name=name, align_bytes=64)
            return keep.tile(shape, dtype, name=name, tag=slot, bufs=1, align_bytes=64)

        def bank(i, name, shape):
            return psum.tile(shape, F32, name=name, tag="bank%d" % i, bufs=1)

        def zero(engine, tile):
            engine.memset(tile[:].bitcast(I32), 0)

        def load_planes_packed(queue, tile, scales):
            for q in range(QUADS):
                queue.dma_start(
                    out=tile[32 * q : 32 * q + 8, :].bitcast(I32),
                    in_=scales[:, 4 * q : 4 * q + 4, :].bitcast(I32),
                )

        def load_planes_spread(tile, scales):
            for r in range(4):
                nc.sync.dma_start(
                    out=tile[r:P:APART, :].bitcast(I32),
                    in_=scales[:, r:16:4, :].bitcast(I32).rearrange("a q n -> q a n"),
                )

        def lower_second_plane(plane, both):
            nc.sync.dma_start(out=plane[0:LIVE, :].bitcast(I32), in_=both[APART : APART + LIVE, :].bitcast(I32))

        def load_words(tile, words):
            nc.sync.dma_start(out=tile[:].bitcast(I32), in_=words.rearrange("p t i -> p (t i)").bitcast(I32))

        offs_t = keep.tile([P, S // 16], U16, name="offs_t")
        pos_t = keep.tile([P, M // 16], U16, name="pos_t")
        offs2_t = keep.tile([P, M // 16], U16, name="offs2_t")

        tab_sc = sb("tab_sc", [P, T], U8, "tab_sc")
        wc_sc_raw = sb("wc_sc_raw", [P, 2 * H], U8, "wc_sc_raw")
        tab2_sc = sb("tab2_sc", [P, T], U8, "tab2_sc")
        v_sc = [sb("v_sc%d" % a, [P, S], U8) for a in range(2)]
        v2_sc = [sb("v2_sc%d" % a, [P, M], U8) for a in range(2)]
        wo_sc = sb("wo_sc", [P, N], U8)
        zero(nc.gpsimd, tab_sc)
        for tile in (wc_sc_raw, tab2_sc, v_sc[1], v2_sc[1], wo_sc):
            zero(nc.vector, tile)

        nc.sync.dma_start(offs_t[:], offs)
        nc.sync.dma_start(pos_t[:], pos1)
        load_planes_spread(tab_sc, tab_scales)
        wc_raw = [sb("wc_raw%d" % b, [P, 2 * 2 * PASS], U8, "wc_raw%d" % b) for b in range(2)]

        def load_wc(b):
            nc.sync.dma_start(
                out=wc_raw[b][:].bitcast(I32).rearrange("p (a c) -> p a c", a=2),
                in_=wc_words[:, :, 2 * PASS * b : 2 * PASS * (b + 1)].bitcast(I32).rearrange("a p c -> p a c"),
            )

        def load_wc_scales(queue):
            for r in range(4):
                queue.dma_start(
                    out=wc_sc_raw[r:P:32, :].bitcast(I32).rearrange("q (a c) -> q a c", a=2),
                    in_=wc_scales[:, r:16:4, :].bitcast(I32).rearrange("a q c -> q a c"),
                )

        wf_raw = {}

        def load_wf(a, b):
            wf_raw[a, b] = sb("wf_raw%d%d" % (a, b), [P, PACK, PASS], F32, "wf%d%d" % (a, b))
            nc.sync.dma_start(
                out=wf_raw[a, b][:],
                in_=wf[PASS * a : PASS * (a + 1), PASS * b : PASS * (b + 1)].rearrange("(p j) c -> p j c", j=PACK),
            )

        tab_w = [sb("tab_w%d" % a, [P, T], U32, "tab%d" % a) for a in range(2)]
        tab2_w = [sb("tab2_w%d" % a, [P, T], U32, "tab2%d" % a) for a in range(2)]
        level_t = sb("level_t", [P, 2, PACK], F32)
        fade_t = sb("fade_t", [P, 2, PACK], F32)

        def load_factor(tile, values):
            nc.sync.dma_start(out=tile[:], in_=values.rearrange("(b p t) -> p b t", b=2, t=PACK))

        def gather_tab2_scales():
            nc.vector.tensor_copy(v2_sc[0][:], tab2_sc[:].indirect(offs2_t[:]))
            lower_second_plane(v2_sc[1], v2_sc[0])

        def gather_tab_scales():
            nc.vector.tensor_copy(v_sc[0][:], tab_sc[:].indirect(offs_t[:]))
            lower_second_plane(v_sc[1], v_sc[0])

        load_wc(0)
        load_words(tab_w[0], tab_words[0])
        load_wc_scales(nc.sync)
        load_words(tab_w[1], tab_words[1])
        gather_tab_scales()
        nc.sync.dma_start(offs2_t[:], offs2)
        load_wc(1)
        load_planes_spread(tab2_sc, tab2_scales)
        load_wf(0, 0)
        load_wf(1, 0)
        load_words(tab2_w[0], tab2_words[0])
        gather_tab2_scales()
        load_factor(level_t, level)
        load_wf(0, 1)
        load_wf(1, 1)
        load_words(tab2_w[1], tab2_words[1])
        load_factor(fade_t, fade)

        late = {}

        def load_late():
            load_planes_packed(nc.sync, wo_sc, wo_scales)
            late["wo"] = sb("wo_w", [P, 2 * N], U32, "tab1")
            nc.sync.dma_start(
                out=late["wo"][:].bitcast(I32).rearrange("p (a c) -> p a c", a=2),
                in_=wo_words.rearrange("a p c i -> p a (c i)").bitcast(I32),
            )
            late["base"] = sb("base_t", [P, N // P, M], F32, "tab0")
            nc.sync.dma_start(out=late["base"][:], in_=base.rearrange("(c p) m -> p c m", p=P))

        wc_w = [sb("wc_w%d" % b, [P, 2 * PACK * 2 * P], U8) for b in range(2)]
        wc_sc = {}

        def order_wc_scales(b, pieces):
            wc_sc[b] = sb("wc_sc%d" % b, [P, 2 * PACK * P], U8)
            for t0 in range(0, PACK, PACK // pieces):
                ts = slice(t0, t0 + PACK // pieces)
                nc.gpsimd.tensor_copy(
                    wc_sc[b][:].rearrange("p (t a m) -> p t a m", a=2, t=PACK)[:, ts],
                    wc_sc_raw[:].rearrange("p (a b m t) -> p b t a m", a=2, b=2, t=PACK)[:, b, ts],
                )

        def order_wc_words(b):
            nc.vector.tensor_copy(
                wc_w[b][:].bitcast(U16).rearrange("p (a t m) -> p a t m", a=2, t=PACK),
                wc_raw[b][:].bitcast(U16).rearrange("p (a m t) -> p a t m", a=2, t=PACK),
            )

        def order_wc_words_gpsimd(b, pieces):
            for t0 in range(0, PACK, PACK // pieces):
                ts = slice(t0, t0 + PACK // pieces)
                nc.gpsimd.tensor_copy(
                    wc_w[b][:].rearrange("p (t a m e) -> p t a m e", a=2, t=PACK, e=2)[:, ts],
                    wc_raw[b][:].rearrange("p (a m t e) -> p t a m e", a=2, t=PACK, e=2)[:, ts],
                )

        v_w = {}

        def gather_tab(a, h, slot=None):
            v_w[a, h] = sb("v_w%d%d" % (a, h), [P, BANK], U32, slot)
            nc.vector.tensor_copy(v_w[a, h][:], tab_w[a][:].indirect(offs_t[:, 32 * h : 32 * (h + 1)]))

        def gather_tab_whole(a):
            whole = sb("v_w%d" % a, [P, S], U32)
            nc.vector.tensor_copy(whole[:], tab_w[a][:].indirect(offs_t[:]))
            for h in range(2):
                v_w[a, h] = whole[:, BANK * h : BANK * (h + 1)]

        coarse = [sb("coarse%d" % k, [P, S], F32, "coarse%d" % k) for k in range(SLICES)]

        def coarse_half(k, h):
            b, t = divmod(k, PACK)
            acc = bank((2 * k + h) % 4, "acc", [P, BANK])
            cols = slice(BANK * h, BANK * (h + 1))
            for a in range(2):
                place = 2 * t + a
                nc.tensor.matmul_mx(
                    out=acc[:],
                    lhsT=wc_w[b][:, 2 * P * place : 2 * P * (place + 1)].bitcast(FP4X4),
                    lhsT_scale=wc_sc[b][:, P * place : P * (place + 1)],
                    rhs=v_w[a, h][:].bitcast(FP8X4),
                    rhs_scale=v_sc[a][:, cols],
                    start=(a == 0),
                    stop=(a == 1),
                )
            nc.scalar.activation(coarse[k][:, cols], acc[:], ACT.Copy)

        wf_w, wf_sc = {}, {}
        wf_bf = [sb("wf_bf%d" % b, [P, 2 * PACK * PASS], BF16, "wf_bf%d" % b) for b in range(2)]

        def round_wf_scalar(a, b, u):
            nc.scalar.copy(
                wf_bf[b][:].rearrange("p (a u e m j) -> p a u m j e", a=2, u=2, e=2, j=PACK)[:, a, u],
                wf_raw[a, b][:].rearrange("p j (m u e) -> p u m j e", u=2, e=2)[:, u],
            )

        def round_wf_gpsimd(a, b, u):
            nc.gpsimd.tensor_scalar(
                wf_bf[b][:].rearrange("p (a u e m j) -> p a u m e j", a=2, u=2, e=2, j=PACK)[:, a, u],
                wf_raw[a, b][:].rearrange("p j (m u e) -> p u m e j", u=2, e=2)[:, u],
                1.0, 0.0, ALU.mult, ALU.add,
            )

        def quantize_wf(b, slot):
            wf_w[b] = sb("wf_w%d" % b, [P, 2, PASS], U32, slot)
            wf_sc[b] = sb("wf_sc%d" % b, [P, 2 * PASS], U8)
            nc.vector.quantize_mx(
                out=wf_w[b][:].rearrange("p a c -> p (a c)").bitcast(FP8X4), scales=wf_sc[b][:], in_=wf_bf[b][:]
            )

        v2_w = [sb("v2_w%d" % a, [P, M], U32) for a in range(2)]

        def gather_tab2(a):
            nc.vector.tensor_copy(v2_w[a][:], tab2_w[a][:].indirect(offs2_t[:]))

        picked, scaled, fine, diff, step = {}, {}, {}, {}, {}

        def carve(name, slot, *parts):
            whole = sb(name, [P, sum(rows for store, key, rows in parts), M], F32, slot)
            at = 0
            for store, key, rows in parts:
                store[key] = whole[:, at : at + rows, :]
                at = at + rows

        alone = {}

        def one_pick(k):
            return alone[k][:, 0, :] if k in alone else picked[k // 2][:, k % 2, :]

        def pick(k):
            nc.vector.tensor_copy(one_pick(k), coarse[k][:].indirect(pos_t[:]))

        def scale_pick(k):
            b, t = divmod(k, PACK)
            nc.gpsimd.tensor_scalar(
                scaled[k][:, 0, :], one_pick(k), level_t[:, b, t : t + 1], 0.0, ALU.mult, ALU.add
            )

        def scale_pick_scalar(k):
            b, t = divmod(k, PACK)
            nc.scalar.activation(scaled[k][:, 0, :], one_pick(k), ACT.Copy, scale=level_t[:, b, t : t + 1])

        def fine_passes(g, h, a, i=None):
            if a == 0:
                fine[g, h] = bank(i, "fine", [P, 2, HALF])
            cols_m = slice(HALF * h, HALF * (h + 1))
            for e in range(2):
                b, t = divmod(2 * g + e, PACK)
                nc.tensor.matmul_mx(
                    out=fine[g, h][:, e, :],
                    lhsT=wf_w[b][:, a, P * t : P * (t + 1)].bitcast(FP8X4),
                    lhsT_scale=wf_sc[b][:, PASS * a + P * t : PASS * a + P * (t + 1)],
                    rhs=v2_w[a][:, cols_m].bitcast(FP8X4),
                    rhs_scale=v2_sc[a][:, cols_m],
                    start=(a == 0 and e == 0),
                    stop=(a == 1 and e == 1),
                )

        def difference(g, h):
            cols = slice(HALF * h, HALF * (h + 1))
            both = diff[g, h][:, 0, :].rearrange("p (e m) -> p e m", e=2)
            if g in picked:
                nc.vector.tensor_tensor(both, fine[g, h][:], picked[g][:, :, cols], ALU.subtract)
            else:
                for e in range(2):
                    nc.vector.tensor_tensor(both[:, e, :], fine[g, h][:, e, :], one_pick(2 * g + e)[:, cols], ALU.subtract)
            nc.scalar.activation(step[g, h][:, 0, :], diff[g, h][:, 0, :], ACT.Tanh)

        z_rows, z_bf, z_w, z_sc = {}, {}, {}, {}

        def blend(b, m0, n, slot=None):
            z_rows[b, m0] = sb("z_rows%d%d" % (b, m0), [P, PACK, n * P], BF16, slot)
            h, within = divmod(P * m0, HALF)
            for t in range(PACK):
                nc.vector.scalar_tensor_tensor(
                    z_rows[b, m0][:, t, :], step[2 * b + t // 2, h][:, 0, HALF * (t % 2) + within : HALF * (t % 2) + within + n * P],
                    fade_t[:, b, t : t + 1], scaled[PACK * b + t][:, 0, P * m0 : P * (m0 + n)], ALU.mult, ALU.add,
                )

        def weave(copy, b, m0, n, slot=None):
            z_bf[b, m0] = sb("z_bf%d%d" % (b, m0), [P, n * P * PACK], BF16, slot)
            copy(
                z_bf[b, m0][:].rearrange("p (c i t) -> p c t i", i=4, t=PACK),
                z_rows[b, m0][:].rearrange("p t (c i) -> p c t i", i=4),
            )

        def quantize_z(b, m0, n, slot=None):
            z_w[b, m0] = sb("z_w%d%d" % (b, m0), [P, n * P], U32, slot)
            z_sc[b, m0] = sb("z_sc%d%d" % (b, m0), [P, n * P], U8)
            nc.vector.quantize_mx(out=z_w[b, m0][:].bitcast(FP8X4), scales=z_sc[b, m0][:], in_=z_bf[b, m0][:])

        height = {}

        def height_passes(b, source, m0, n, banks):
            per = BANK // (n * P)
            cols = slice(P * (m0 - source), P * (m0 - source + n))
            for c in range(N // P):
                if b == 0 and c % per == 0:
                    height[m0, c // per] = bank(banks[c // per], "height", [P, per, n * P])
                nc.tensor.matmul_mx(
                    out=height[m0, c // per][:, c % per, :],
                    lhsT=late["wo"][:, N * b + P * c : N * b + P * (c + 1)].bitcast(FP8X4),
                    lhsT_scale=wo_sc[4 * b : P, P * c : P * (c + 1)],
                    rhs=z_w[b, source][:, cols].bitcast(FP8X4),
                    rhs_scale=z_sc[b, source][:, cols],
                    start=(b == 0 and c % per == 0),
                    stop=(b == 1 and c % per == per - 1),
                )

        results = {}

        def finish(m0, n, i, first, count):
            per = BANK // (n * P)
            cols = slice(P * m0, P * (m0 + n))
            c0 = per * i + first
            result = results[m0, i][:, 0, :].rearrange("p (c m) -> p c m", c=per)[:, first : first + count, :]
            nc.vector.tensor_tensor(
                result, height[m0, i][:, first : first + count, :], late["base"][:, c0 : c0 + count, cols], ALU.add
            )
            nc.sync.dma_start(out=out[P * c0 : P * (c0 + count), cols].rearrange("(i p) m -> p i m", p=P), in_=result)

        order_wc_words_gpsimd(0, 1)
        order_wc_scales(0, 2)
        order_wc_scales(1, 1)
        order_wc_words_gpsimd(1, 2)
        gather_tab_whole(0)
        gather_tab(1, 0)
        coarse_half(0, 0)
        gather_tab(1, 1)
        coarse_half(0, 1)
        load_late()
        for k in range(1, SLICES):
            coarse_half(k, 0)
            coarse_half(k, 1)
        round_wf_gpsimd(0, 0, 0)
        round_wf_gpsimd(0, 0, 1)
        round_wf_gpsimd(1, 0, 0)
        round_wf_scalar(1, 0, 1)
        carve("picked0", "tab2_sc", (picked, 0, 2), (picked, 1, 2))
        pick(0)
        pick(1)
        carve("picked1", "picked1", (picked, 2, 2))
        for k in range(2, 5):
            pick(k)
        gather_tab2(0)
        pick(5)
        carve("pick6", "pick6", (alone, 6, 1))
        pick(6)
        quantize_wf(0, "coarse5")
        carve("after_wf0", "wf_bf0", (alone, 7, 1), *[(scaled, k, 1) for k in range(3)])
        pick(7)
        for k in range(3):
            scale_pick(k)
        for a in range(2):
            for u in range(2):
                round_wf_scalar(a, 1, u)
        carve("after_round", "wf11", (scaled, 3, 1))
        scale_pick_scalar(3)
        gather_tab2(1)
        for a in range(2):
            for h in range(2):
                for g in range(2):
                    fine_passes(g, h, a, 4 + 2 * h + g)
        quantize_wf(1, "tab21")
        carve("after_wf1", "wf_bf1", *[(scaled, k, 1) for k in range(PACK, SLICES)])
        for k in range(PACK, SLICES):
            scale_pick(k)
        for h in range(2):
            for g in range(2):
                for a in range(2):
                    fine_passes(2 + g, h, a, 2 * h + g)
        carve("diffs0", "diffs0", (diff, (0, 0), 1), (diff, (1, 0), 1), (diff, (0, 1), 1), (diff, (1, 1), 1))
        carve("steps0", "wf00", (step, (0, 0), 1), (step, (1, 0), 1), (step, (0, 1), 1), (step, (1, 1), 1))
        carve("diffs1", "wf01", (diff, (2, 0), 1), (diff, (3, 0), 1), (diff, (2, 1), 1), (diff, (3, 1), 1))
        carve("steps1", "wf10", (step, (2, 0), 1), (step, (3, 0), 1), (step, (2, 1), 1), (step, (3, 1), 1))
        for g, h in ((0, 0), (1, 0), (0, 1), (1, 1), (2, 0), (3, 0)):
            difference(g, h)
        blend(0, 0, 2)
        weave(nc.scalar.copy, 0, 0, 2, "z_bf00")
        blend(1, 0, 2)
        weave(nc.scalar.copy, 1, 0, 2)
        difference(2, 1)
        difference(3, 1)
        blend(0, 2, 2)
        weave(nc.scalar.copy, 0, 2, 2)
        quantize_z(0, 0, 2)
        quantize_z(1, 0, 2)
        height_passes(0, 0, 0, 2, (4, 5))
        height_passes(1, 0, 0, 2, (4, 5))
        blend(1, 2, 1, "z_bf00")
        weave(nc.scalar.copy, 1, 2, 1)
        blend(1, 3, 1, "z_rows13")
        quantize_z(0, 2, 2)
        height_passes(0, 2, 2, 1, (6,))
        height_passes(0, 2, 3, 1, (7,))
        weave(nc.vector.tensor_copy, 1, 3, 1)
        quantize_z(1, 2, 1)
        height_passes(1, 2, 2, 1, (6,))
        quantize_z(1, 3, 1)
        height_passes(1, 3, 3, 1, (7,))
        carve("results0", "z_rows13", (results, (0, 0), 1), (results, (0, 1), 1))
        carve("results1", "results1", (results, (2, 0), 1), (results, (3, 0), 1))
        finish(0, 2, 0, 0, 2)
        finish(0, 2, 1, 0, 2)
        finish(2, 1, 0, 0, 4)
        finish(3, 1, 0, 0, 2)
        finish(3, 1, 0, 2, 2)
